import numpy as np, ml_dtypes
CORES = [2,6,10,14,18,22,26,30]
N = 8
import mx_ref
BF = ml_dtypes.bfloat16
def entries(a):
    return np.ascontiguousarray(a.T).reshape(-1)
def table(e):
    return np.ascontiguousarray(np.reshape(e, (-1, 16)).T).astype(np.int32)
def cols(t, e):
    v = np.concatenate([t.reshape(128, -1, 4), np.zeros((128, 1, 4), BF)], axis=1)
    return np.ascontiguousarray(v[:, e]).reshape(128, -1)
def cut(t, i, w=512):
    return t[:, w * i:w * i + w]
def f(rng, *shape):
    return mx_ref.flush((rng.standard_normal(shape, dtype=np.float32) * np.exp2(rng.integers(-2, 3, shape[:-1] + (1,)))).astype(BF))
def wide(rng, *shape, cols=0):
    v = rng.standard_normal(shape, dtype=np.float32) * np.exp2(rng.integers(-12, 13, shape)).astype(np.float32)
    if cols: v *= np.repeat(np.exp2(rng.integers(-cols, cols + 1, shape[:-2] + (1, shape[-1] // 4))) * (rng.random(shape[:-2] + (1, shape[-1] // 4)) > 0.0625), 4, axis=-1).astype(np.float32)
    return mx_ref.flush(v.astype(BF))
K, B, R, O, CO = 256, 12, 5, 2, 56
def others(d):
    return [s for s in range(N) if s != d]
def numbers_of(a):
    return np.stack([entries(e) for e in a]).reshape(N, R, N, B)
def batch(tab, cs, t, d):
    return np.concatenate([cols(tab[s], cs[s, t, d]) for s in others(d)], axis=1)
def passes(u, new):
    return int(np.sum(mx_ref.matmul(mx_ref.quantize(u), mx_ref.quantize(new))[0] >= 0))
def write(tab, new, keys):
    tab.reshape(128, K, 4)[:, keys] = new.reshape(128, -1, 4)
def level(rng, n, rule, must):
    if rule == "all": return min(n)
    if rule == "none": return max(n) + 1
    if rule == "edge": return max(n)
    v = min(n, key=lambda a: abs(2 * sum(b >= a for b in n) - N))
    low = max([a for a in n if a < v], default=v - 1)
    h = int(rng.integers(low + 1, v + 1))
    return min(h, n[must]) if rule == "chain" else h
def draw_key(rng, at, got, d):
    for _ in range(1000):
        k = int(rng.integers(0, K)); q = divmod(int(at[k]), K)[0]
        if q == d or got[at[k]] or got.reshape(N, K)[q].sum() < CO:
            got[at[k]] = True
            return k
    raise RuntimeError("no key")
def draw_new(rng, at, got, d, q):
    k = np.flatnonzero((at >= q * K) & (at < q * K + K) & ~got[at])
    if len(k) == 0 or got.reshape(N, K)[q].sum() >= CO: return draw_key(rng, at, got, d)
    k = int(rng.choice(k)); got[at[k]] = True
    return k
def game(rng, x, u, rule):
    cs, cd, thr = np.full((N, R, N, B), -1), np.full((N, R, N, B), -1), np.zeros(16, int)
    tab, at = np.array(x, order="C"), np.arange(N * K).reshape(N, K)
    got = np.zeros((N, N * K), bool)
    p, hold, done = rng.permutation(N), rng.permutation(K)[:B], 0
    one, told = int(rng.integers(0, R)), {"all": 0, "none": (N - 1) * B + 1, "chain": (N - 1) * B}
    if rule == "chain":
        got[:, p[0] * K + hold] = True
        u[int(p[(one + 1) % N])] = 0
    for t in range(R):
        a, e = int(p[t % N]), int(p[(t + 1) % N])
        for d in range(N):
            cd[d, t, others(d)] = rng.permutation(K)[:(N - 1) * B].reshape(N - 1, B)
            for s in others(d):
                if rule == "chain" and (s, d) == (a, e): cs[s, t, d] = hold
                elif rule == "all" and d == p[0]: cs[s, t, d] = [draw_new(rng, at[s], got[d], d, int(p[1])) for j in range(B)]
                else: cs[s, t, d] = [draw_key(rng, at[s], got[d], d) for j in range(B)]
        new = [batch(tab, cs, t, d) for d in range(N)]
        src = [np.concatenate([at[s, cs[s, t, d]] for s in others(d)]) for d in range(N)]
        n = [passes(u[d], new[d]) for d in range(N)]
        thr[t] = told[rule] if t == one and rule in told else level(rng, n, rule, e)
        for d in range(N):
            if n[d] >= thr[t]:
                keys = cd[d, t, others(d)].reshape(-1)
                write(tab[d], new[d], keys); at[d, keys] = src[d]; done += 1
        hold = cd[e, t, a]
    return cs, cd, thr, done, int(got[p[0]].reshape(N, K)[p[1]].sum())
def make(rng, rule="half", x=None):
    if x is None: x = f(rng, N, 128, 4 * K)
    u = np.zeros((N, 128, 512), BF); u[:, :, :4] = f(rng, N, 128, 4)
    w = f(rng, N, 128, 512 * R * O)
    for _ in range(50):
        cs, cd, thr, done, most = game(rng, x, u, rule)
        if (rule != "half" or N * R <= 3 * done <= 2 * N * R) and (rule != "all" or most == CO):
            return {"x": x, "u": u, "w": w, "cs": np.stack([table(e.reshape(-1)) for e in cs]), "cd": np.stack([table(e.reshape(-1)) for e in cd]), "thr": np.stack([table(thr) for r in range(N)])}
    raise RuntimeError("no draw")
def setup_inputs(rng):
    return make(rng)
def setup_inputs_all(rng):
    return make(rng, "all")
def setup_inputs_none(rng):
    return make(rng, "none")
def setup_inputs_edge(rng):
    return make(rng, "edge")
def setup_inputs_chain(rng):
    return make(rng, "chain")
def setup_inputs_spread(rng):
    x = np.array(wide(rng, N, 128, 4 * K, cols=6))
    x[np.abs(x.astype(np.float32)) < 2.0 ** -30] = 0
    return make(rng, "half", x)
def check_inputs(d):
    b = []
    for name in ("x", "u", "w"):
        v = np.abs(np.asarray(d[name]).astype(np.float32))
        if not (np.isfinite(v) & ((v == 0) | ((v >= 2.0 ** -30) & (v <= 2.0 ** 30)))).all(): b.append(name + ": a value that isn't finite, or neither zero nor 2**-30 to 2**30 in size")
    cs, cd = numbers_of(d["cs"]), numbers_of(d["cd"])
    for r in range(N):
        for t in range(R):
            if (cs[r, t, r] != -1).any() or (cd[r, t, r] != -1).any(): b.append("a rank's own part isn't -1")
            k, e = cs[r, t, others(r)], cd[r, t, others(r)].reshape(-1)
            if k.min() < 0 or k.max() >= K: b.append("cs")
            if e.min() < 0 or e.max() >= K or len(set(e.tolist())) != len(e): b.append("cd")
        h = entries(d["thr"][r])
        if (h != entries(d["thr"][0])).any(): b.append("thr isn't the same on every rank")
        if h.min() < 0 or h.max() > (N - 1) * B + 1 or (h[R:] != 0).any(): b.append("thr")
    if (np.asarray(d["u"])[:, :, 4:].astype(np.float32) != 0).any(): b.append("u")
    if b: return b
    tab, at = np.array(d["x"], order="C"), np.arange(N * K).reshape(N, K)
    got = np.zeros((N, N * K), bool)
    for t in range(R):
        new = [batch(tab, cs, t, r) for r in range(N)]
        src = [np.concatenate([at[s, cs[s, t, r]] for s in others(r)]) for r in range(N)]
        for r in range(N):
            if passes(d["u"][r], new[r]) >= entries(d["thr"][r])[t]:
                keys = cd[r, t, others(r)].reshape(-1)
                write(tab[r], new[r], keys); at[r, keys] = src[r]; got[r, src[r]] = True
    for r in range(N):
        for q in others(r):
            if got[r].reshape(N, K)[q].sum() > CO: b.append("too many columns of one rank are written on another")
    return b
def reference(x, u, w, cs, cd, thr):
    cs, cd = numbers_of(cs), numbers_of(cd)
    tab = np.array(x, order="C")
    y = np.zeros((N, 128, R * O * K), np.float32)
    for t in range(R):
        new = [batch(tab, cs, t, d) for d in range(N)]
        for d in range(N):
            if passes(u[d], new[d]) >= entries(thr[d])[t]: write(tab[d], new[d], cd[d, t, others(d)].reshape(-1))
            q = mx_ref.quantize(tab[d])
            for o in range(O):
                i = t * O + o
                y[d][:, K * i:K * i + K] = mx_ref.matmul(mx_ref.quantize(cut(w[d], i)), q)
    return {"y": y}

@@ -1,0 +1,359 @@
+import numpy as np
+from concourse.bass import DstId, RemoteDMATransfer
+from concourse.mybir import dt, AluOpType, AxisListType, ActivationFunctionType
+
+N, K, B, R, O = 8, 256, 12, 5, 2
+NB = N * B
+NEW = (N - 1) * B
+LC = NB // 16
+TC = K // 16
+AL = R * LC
+WIN = K + 16
+
+CODE, BYTE = "float8_e4m3fn_x4", "uint8"
+SCRATCH = {
+    "xt": ("sbuf", [128, 4 * K], "bfloat16"),
+    "ut": ("sbuf", [128, 512], "bfloat16"),
+    "wt": ("sbuf", [128, 512 * R * O], "bfloat16"),
+    "csl": ("sbuf", [128, AL], "int32"),
+    "cdl": ("sbuf", [128, AL], "int32"),
+    "thr1": ("sbuf", [1, 16], "int32"),
+    "thri": ("sbuf", [128, 16], "int32"),
+    "thrf": ("sbuf", [128, 16], "float32"),
+    "csu": ("sbuf", [128, AL], "uint16"),
+    "cdo": ("sbuf", [128, AL], "uint16"),
+    "own1": ("sbuf", [128, AL], "float32"),
+    "own2": ("sbuf", [128, AL], "float32"),
+    "cdf": ("sbuf", [128, AL], "float32"),
+    "trash": ("sbuf", [128, AL], "float32"),
+    "trash2": ("sbuf", [128, AL], "float32"),
+    "pp": ("sbuf", [128, 2], "int32"),
+    "p16": ("sbuf", [128, 2], "int32"),
+    "p16f": ("sbuf", [128, 2], "float32"),
+    "run": ("sbuf", [128, 640], "float32"),
+    "mask": ("sbuf", [128, 384], "float32"),
+    "seg": ("sbuf", [128, 640], "float32"),
+    "jc": ("sbuf", [128, TC], "float32"),
+    "jl": ("sbuf", [128, TC], "float32"),
+    "vrow": ("sbuf", [128, NB], "float32"),
+    "inv": ("sbuf", [128, R * WIN], "float32"),
+    "lists": ("sbuf", [128, AL + TC], "float32"),
+    "zeros": ("sbuf", [128, 8], "uint16"),
+    "uc": ("sbuf", [128, 128], CODE), "us": ("sbuf", [128, 128], BYTE),
+    "vc": ("sbuf", [128, 128], CODE), "vs": ("sbuf", [128, 128], BYTE),
+    "wc": ("sbuf", [128, 128 * R * O], CODE), "ws": ("sbuf", [128, 128 * R * O], BYTE),
+    "ttc": ("sbuf", [128, 2 * K], CODE), "tts": ("sbuf", [128, 2 * K], BYTE),
+    "ty": ("sbuf", [128, R * O * K], "float32"),
+    "acc": ("psum", [128, 1024], "float32"),
+    "prod": ("psum", [128, 2048], "float32"),
+    "fcf": ("sbuf", [128, TC], "float32"),
+    "fcu": ("sbuf", [128, TC], "uint16"),
+    "pkl": ("sbuf", [128, TC], "uint16"),
+}
+for _k in range(R + 1):
+    SCRATCH["pc%d" % _k] = ("sbuf", [128, K + NEW * _k], CODE)
+    SCRATCH["ps%d" % _k] = ("sbuf", [128, K + NEW * _k], BYTE)
+for _t in range(R):
+    SCRATCH["sc%d" % _t] = ("sbuf", [128, NB], CODE)
+    SCRATCH["ss%d" % _t] = ("sbuf", [128, NB], BYTE)
+    SCRATCH["val%d" % _t] = ("sbuf", [128, NB], "float32")
+    SCRATCH["lin%d" % _t] = ("sbuf", [128, 640], "float32")
+    SCRATCH["sum%d" % _t] = ("sbuf", [128, 640], "float32")
+    SCRATCH["bit%d" % _t] = ("sbuf", [128, NEW], "bfloat16")
+    SCRATCH["num%d" % _t] = ("sbuf", [128, 4], "float32")
+    SCRATCH["tmp%d" % _t] = ("sbuf", [128, AL + TC], "float32")
+    SCRATCH["lu%d" % _t] = ("sbuf", [128, AL + TC], "uint16")
+    if _t:
+        SCRATCH["cc%d" % _t] = ("sbuf", [128, 2 * NB], CODE)
+        SCRATCH["cs_%d" % _t] = ("sbuf", [128, 2 * NB], BYTE)
+        SCRATCH["ncf%d" % _t] = ("sbuf", [128, LC], "float32")
+        SCRATCH["ncu%d" % _t] = ("sbuf", [128, LC], "uint16")
+        SCRATCH["pk%d" % _t] = ("sbuf", [128, LC], "uint16")
+    if _t < R - 2 or _t == R - 1:
+        SCRATCH["tc%d" % _t] = ("sbuf", [128, K], CODE)
+        SCRATCH["ts%d" % _t] = ("sbuf", [128, K], BYTE)
+
+SEMAPHORES = ["vq", "aq", "pq", "gq", "snt", "lx0", "lx1", "lc0", "lc1", "ld0", "ld1", "lu", "lt", "lw0", "lw1"]
+for _t in range(R):
+    SEMAPHORES += ["arrc%d" % _t, "arrs%d" % _t, "yo%d" % _t]
+for _k in range(2, R + 1):
+    SEMAPHORES += ["cp%d" % _k]
+SEMAPHORES += ["yp"]
+
+
+def deal(topo, cores, s):
+    src = cores[s]
+    home, off = [], []
+    for d in range(len(cores)):
+        if d != s:
+            (home if topo.chip(cores[d]) == topo.chip(src) else off).append(d)
+    near = lambda d: topo.mates(topo.chip(src), topo.chip(cores[d])) or topo.same_plane(topo.chip(src), topo.chip(cores[d]))
+    off = [d for d in off if not near(d)] + [d for d in off if near(d)]
+    eng = topo.engines(src, cores[off[0]])
+    two = len(eng) - len(off)
+    half = 2 * two
+    codes, scales = {}, {}
+    for i, d in enumerate(off):
+        codes[d] = [eng[2 * i], eng[2 * i + 1]] if i < two else [eng[half + i - two]]
+    one = off[two:] + off[:two]
+    for i, d in enumerate(one):
+        k = len(off) - two
+        scales[d] = [eng[i]] if i < k else [eng[k + 2 * (i - k)], eng[k + 2 * (i - k) + 1]]
+    for d in home:
+        rest = [e for e in topo.engines(src, cores[d]) if e not in eng]
+        pick = rest[::max(1, len(rest) // 2)][:2]
+        codes[d], scales[d] = pick, pick
+    bits = lambda m: {d: sum(1 << e for e in m[d]) for d in m}
+    return bits(codes), bits(scales)
+
+
+def rank_program(g, core, T, topo):
+    r = T.rank_of(core)
+    if r is None:
+        return
+    cores = list(T.cores)
+    A, F = AluOpType, ActivationFunctionType
+    plans = [deal(topo, cores, s) for s in range(N)]
+    ones = lambda m: bin(m).count("1")
+
+    total, W, RD = {}, {}, {}
+    qs = {}
+    for name, eng, sem in (("v", g.vector, "vq"), ("a", g.scalar, "aq"), ("p", g.tensor, "pq"), ("g", g, "gq"), ("s", g.sync, None)):
+        qs[name] = {"eng": eng, "sem": sem, "seen": {}}
+
+    def hold(q, toks):
+        need = {}
+        for sem, n in toks:
+            n = total[sem] if n is None else n
+            if qs[q]["seen"].get(sem, 0) < n:
+                need[sem] = max(need.get(sem, 0), n)
+        for sem in sorted(need):
+            qs[q]["eng"].wait_ge(T.sem[sem], need[sem])
+            qs[q]["seen"][sem] = need[sem]
+
+    def order(q, rd, wr):
+        toks = []
+        for k in rd:
+            toks += W[k]
+        for k in wr:
+            toks += W.get(k, []) + RD.get(k, [])
+        hold(q, toks)
+
+    def note(tok, rd, wr):
+        for k in rd:
+            RD.setdefault(k, []).append(tok)
+        for k in wr:
+            W[k] = [tok]
+            RD[k] = []
+
+    def do(q, make, rd, wr):
+        order(q, rd, wr)
+        sem = qs[q]["sem"]
+        make(qs[q]["eng"]).then_inc(T.sem[sem], 1)
+        total[sem] = total.get(sem, 0) + 1
+        note((sem, total[sem]), rd, wr)
+
+    def dma(q, sem, out, in_, rd, wr):
+        order(q, rd, [])
+        qs[q]["eng"].dma_start(out, in_).then_inc(T.sem[sem], 16)
+        total[sem] = total.get(sem, 0) + 16
+        tok = (sem, None)
+        for k in rd:
+            RD.setdefault(k, []).append(tok)
+        for k in wr:
+            if tok not in W.setdefault(k, []):
+                W[k].append(tok)
+
+    for t in range(R):
+        for h, nm in ((0, "c"), (1, "s")):
+            sem = "arr%s%d" % (nm, t)
+            total[sem] = sum(ones(plans[s][h][r]) for s in range(N) if s != r)
+            W["land%s%d" % (nm, t)] = [(sem, None)]
+
+    h = 2 * K
+    dma("s", "lx0", T.xt[:, 0:h], T.x[:, 0:h], [], ["x"])
+    dma("a", "lx1", T.xt[:, h:2 * h], T.x[:, h:2 * h], [], ["x"])
+    for i in range(8):
+        q, n = ("s", "0") if i < 4 else ("a", "1")
+        dma(q, "lc" + n, T.csl[16 * i:16 * i + 16, :], T.cs[:, :], [], ["cs"])
+    dma("s", "lu", T.ut[:, :], T.u[:, :], [], ["u"])
+    for i in range(8):
+        q, n = ("s", "0") if i < 4 else ("a", "1")
+        dma(q, "ld" + n, T.cdl[16 * i:16 * i + 16, :], T.cd[:, :], [], ["cd"])
+    dma("s", "lt", T.thr1[0:1, :], T.thr[:, :], [], ["thr1"])
+    hw = 256 * R * O
+    dma("s", "lw0", T.wt[:, 0:hw], T.w[:, 0:hw], [], ["w"])
+    dma("s", "lw1", T.wt[:, hw:2 * hw], T.w[:, hw:2 * hw], [], ["w"])
+
+    do("v", lambda e: e.memset(T.inv[:, :], 0.0), [], ["inv%d" % t for t in range(R)])
+    do("v", lambda e: e.memset(T.zeros[:, :], 0), [], ["zeros"])
+    fl = {"allow_small_or_imprecise_dtypes": True}
+    do("g", lambda e: e.iota(T.pp[:, 0:1], [[0, 1]], 0, 1), [], ["pp"])
+    do("g", lambda e: e.iota(T.trash[:, :], [[0, R], [16, LC]], K + 1 - B * r, 0, **fl), [], ["trash"])
+    do("g", lambda e: e.iota(T.jc[:, :], [[16, TC]], 0, 0, **fl), [], ["jc"])
+    do("g", lambda e: e.iota(T.vrow[:, 0:B * (r + 1)], [[1, B * (r + 1)]], 0, 0, **fl), [], ["vrowa"])
+    W["vrowb"] = []
+    if r < N - 1:
+        do("g", lambda e: e.iota(T.vrow[:, B * (r + 1):NB], [[1, NB - B * (r + 1)]], B * r, 0, **fl), [], ["vrowb"])
+    do("g", lambda e: e.iota(T.run[:, :], [[0, 40], [1, 16]], 0, 0, **fl), [], ["run"])
+
+    def quantise(k):
+        do("v", lambda e: e.quantize_mx(T["pc%d" % k][:, 0:K], T["ps%d" % k][:, 0:K], T.xt[:, :]), ["x"], ["ownc%d" % k, "owns%d" % k])
+
+    def pick(q, out, win, off, rd, wr):
+        if q == "v":
+            do("v", lambda e: e.tensor_copy(T[out[0]][:, out[2]:out[3]].bitcast(dt.uint32), T[win[0]][:, win[2]:win[3]].bitcast(dt.uint32).indirect(off)), rd, wr)
+        else:
+            do("a", lambda e: e.activation(T[out[1]][:, out[2]:out[3]], T[win[1]][:, win[2]:win[3]].indirect(off), F.Copy), rd, wr)
+
+    def send(t):
+        codes, scales = plans[r]
+        for nm, m, scale in (("c", codes, False), ("s", scales, True)):
+            order("g", ["snd%s%d" % (nm, t)], [])
+            moves = []
+            for d in sorted(m):
+                rid, pid, _ring = topo.addr(cores[d])
+                a = K + NEW * t + B * (r - (r > d))
+                src = T["s%s%d" % (nm, t)][:, B * d:B * d + B]
+                dst = T["p%s%d" % (nm, t + 1)][:, a:a + B]
+                if not scale:
+                    src, dst = src.bitcast(dt.uint8), dst.bitcast(dt.uint8)
+                moves.append(RemoteDMATransfer(dst_ids=[DstId(rid=rid, pnc=pid)], dma_engine_mask=m[d], remote_sem=T.sem["arr%s%d" % (nm, t)], src=src, dst=dst))
+            g.remote_dma_fused(moves, local_sem=T.sem.snt)
+            total["snt"] = total.get("snt", 0) + sum(ones(m[d]) for d in m)
+
+    quantise(0)
+    do("v", lambda e: e.tensor_copy(T.csu[:, :], T.csl[:, :]), ["cs"], ["csu"])
+    pick("v", ("sc0", "ss0", 0, NB), ("pc0", "ps0", 0, K), T.csu[:, 0:LC], ["ownc0", "csu"], ["sndc0"])
+    pick("a", ("sc0", "ss0", 0, NB), ("pc0", "ps0", 0, K), T.csu[:, 0:LC], ["owns0", "csu"], ["snds0"])
+    send(0)
+    do("g", lambda e: e.partition_broadcast(T.thri[:, :], T.thr1[0:1, :], 128), ["thr1"], ["thri"])
+
+    quantise(1)
+    do("v", lambda e: e.quantize_mx(T.uc[:, :], T.us[:, :], T.ut[:, :]), ["u"], ["uc", "us"])
+    pick("v", ("vc", "vs", 0, 128), ("uc", "us", 0, 128), T.zeros[:, :], ["uc", "zeros"], ["vc"])
+    pick("a", ("vc", "vs", 0, 128), ("uc", "us", 0, 128), T.zeros[:, :], ["us", "zeros"], ["vs"])
+    pick("v", ("cc1", "cs_1", 0, NB), ("pc1", "ps1", 0, K), T.csu[:, LC:2 * LC], ["ownc1", "csu"], ["ncc1"])
+    pick("a", ("cc1", "cs_1", 0, NB), ("pc1", "ps1", 0, K), T.csu[:, LC:2 * LC], ["owns1", "csu"], ["ncs1"])
+    do("v", lambda e: e.tensor_scalar(T.p16[:, 0:1], T.pp[:, 0:1], 15, None, A.bitwise_and), ["pp"], ["p16"])
+    do("v", lambda e: e.tensor_scalar(T.own1[:, :], T.cdl[:, :], 0.0, None, A.is_lt), ["cd"], ["own1"])
+    do("v", lambda e: e.tensor_copy(T.p16f[:, 0:1], T.p16[:, 0:1]), ["p16"], ["p16f"])
+    do("v", lambda e: e.tensor_scalar(T.lists[:, 0:AL], T.csl[:, :], 0.0, None, A.max), ["cs"], ["lista"])
+    col = T.p16f[:, 0:1]
+    do("v", lambda e: e.tensor_scalar(T.trash2[:, :], T.trash[:, :], col, None, A.add), ["trash", "p16f"], ["trash2"])
+    do("v", lambda e: e.tensor_scalar(T.jl[:, :], T.jc[:, :], col, None, A.add), ["jc", "p16f"], ["jl"])
+    do("v", lambda e: e.tensor_tensor(T.own2[:, :], T.own1[:, :], T.trash2[:, :], A.mult), ["own1", "trash2"], ["own2"])
+    do("v", lambda e: e.tensor_scalar(T.mask[:, :], T.run[:, 0:384], col, None, A.is_equal), ["run", "p16f"], ["mask"])
+    do("v", lambda e: e.tensor_tensor(T.cdf[:, :], T.cdl[:, :], T.own2[:, :], A.add), ["cd", "own2"], ["cdf"])
+    do("v", lambda e: e.tensor_scalar(T.val0[:, :], T.vrow[:, :], float(K), None, A.add), ["vrowa", "vrowb"], ["val0"])
+    do("v", lambda e: e.tensor_copy(T.cdo[:, :], T.cdf[:, :]), ["cdf"], ["cdo"])
+    do("v", lambda e: e.tensor_scalar(T.seg[:, :], T.run[:, :], 0.5, None, A.is_gt), ["run"], ["seg"])
+
+    def later(t):
+        v, s, l, a = "val%d" % t, "sum%d" % t, "lin%d" % t, WIN * t
+        n = NB * (R - 1 - t)
+        if t:
+            do("v", lambda e: e.tensor_scalar(T[v][:, :], T.vrow[:, :], float(K + NEW * t), None, A.add), ["vrowa", "vrowb"], [v])
+        do("v", lambda e: e.tensor_copy(T.inv[:, a:a + WIN].indirect(T.cdo[:, LC * t:LC * t + LC]), T[v][:, :]), [v, "cdo"], ["inv%d" % t])
+        if n:
+            do("v", lambda e: e.tensor_tensor(T[l][:, 0:n], T.inv[:, a:a + WIN].indirect(T.csu[:, LC * (t + 1):AL]), T.mask[:, 0:n], A.mult), ["inv%d" % t, "csu", "mask"], [l + "a"])
+        else:
+            W[l + "a"] = []
+        do("v", lambda e: e.tensor_tensor(T[l][:, n:n + K], T.inv[:, a:a + K], T.mask[:, 0:K], A.mult), ["inv%d" % t, "mask"], [l + "b"])
+        do("v", lambda e: e.tensor_tensor_scan(T[s][:, 0:n + K], T.seg[:, 0:n + K], T[l][:, 0:n + K], 0.0, A.mult, A.add), ["seg", l + "a", l + "b"], [s])
+
+    def newer(t):
+        do("v", lambda e: e.tensor_tensor(T["ncf%d" % t][:, :], T.lists[:, LC * t:LC * t + LC], T["sum%d" % (t - 1)][:, 15:16 * LC:16], A.max), ["lista", "sum%d" % (t - 1)], ["ncf%d" % t])
+        do("v", lambda e: e.tensor_copy(T["ncu%d" % t][:, :], T["ncf%d" % t][:, :]), ["ncf%d" % t], ["ncu%d" % t])
+
+    later(0)
+    newer(1)
+    do("v", lambda e: e.tensor_copy(T.lists[:, AL:AL + TC], T.jl[:, :]), ["jl"], ["listb"])
+    do("v", lambda e: e.tensor_copy(T.thrf[:, :], T.thri[:, :]), ["thri"], ["thrf"])
+    later(1)
+
+    for t in range(R):
+        k, n = t + 1, t + 1
+        end = K + NEW * k
+        base = end - NEW
+        num, bit = T["num%d" % t], "bit%d" % t
+        rest = ["c%d" % k] if t else []
+        held = lambda x: ["own%s%d" % (x, k), "land%s%d" % (x, t)] + (["cp%s%d" % (x, k)] if t else [])
+        if t < R - 1:
+            for nm in ("c", "s"):
+                o, i = T["p%s%d" % (nm, k + 1)][:, K:end], T["p%s%d" % (nm, k)][:, K:end]
+                if nm == "c":
+                    o, i = o.bitcast(dt.uint8), i.bitcast(dt.uint8)
+                dma("s", "cp%d" % (k + 1), o, i, ["land%s%d" % (nm, t)] + (["cp%s%d" % (nm, k)] if t else []), ["cp%s%d" % (nm, k + 1)])
+        if t:
+            y = slice(O * K * (t - 1), O * K * t)
+            dma("s", "yo%d" % (t - 1), T.y[:, y], T.ty[:, y], ["landc%d" % t, "ty%d" % (O * (t - 1)), "ty%d" % (O * (t - 1) + 1)], ["out%d" % (t - 1)])
+        sb = 512 * (t % 2)
+        do("p", lambda e: e.matmul_mx(T.acc[:, sb:sb + 128], T.vc[:, :], T.vs[:, :], T["pc%d" % k][:, end - 128:end], T["ps%d" % k][:, end - 128:end], True, True), ["vc", "vs"] + held("c") + held("s"), ["acc%d" % (t % 2)])
+        if t < R - 1:
+            out, off, ck, cv = ("cc%d" % n, "cs_%d" % n, NB, 2 * NB), T["ncu%d" % n][:, :], "wc%s%d", "ncu%d" % n
+        else:
+            out, off, ck, cv = ("ttc", "tts", K, 2 * K), T.fcu[:, :], "wc%s%d", "fcu"
+        win = ("pc%d" % k, "ps%d" % k, 0, end)
+        pick("v", out, win, off, held("c") + [cv], [ck % ("c", n)])
+        pick("a", out, win, off, held("s") + [cv], [ck % ("s", n)])
+        do("v", lambda e: e.tensor_scalar(T[bit][:, :], T.acc[:, sb + 128 - NEW:sb + 128], 0.0, None, A.is_ge), ["acc%d" % (t % 2)], [bit])
+        do("v", lambda e: e.tensor_reduce(num[:, 0:1], T[bit][:, :], AxisListType.X, A.add), [bit], ["cnt%d" % t])
+        step, width = (NB, LC) if t < R - 1 else (K, TC)
+        do("v", lambda e: e.tensor_scalar(num[:, 1:2], num[:, 0:1], T.thrf[:, t:t + 1], float(step), A.is_ge, A.mult), ["cnt%d" % t, "thrf"], ["shift%d" % t])
+        pkl = T["pk%d" % n] if t < R - 1 else T.pkl
+        do("v", lambda e: e.tensor_scalar(pkl[:, :], T.jl[:, 0:width], num[:, 1:2], None, A.add), ["jl", "shift%d" % t], ["pk%d" % n])
+        if t < R - 1:
+            src, dst = ("cc%d" % n, "cs_%d" % n, 0, 2 * NB), ("sc%d" % n, "ss%d" % n, 0, NB)
+            for q, nm in (("v", "c"), ("a", "s")):
+                pick(q, dst, src, pkl[:, :], ["nc%s%d" % (nm, n), "wc%s%d" % (nm, n), "pk%d" % n], ["snd%s%d" % (nm, n)])
+            send(n)
+            do("v", lambda e: e.tensor_scalar(num[:, 2:3], num[:, 0:1], T.thrf[:, t:t + 1], None, A.is_ge), ["cnt%d" % t, "thrf"], ["com%d" % t])
+            lo = LC * (t + 2)
+            wid = AL + TC - lo
+            tmp, lu, sm = T["tmp%d" % t], T["lu%d" % t], T["sum%d" % t]
+            do("v", lambda e: e.tensor_scalar(tmp[:, 0:wid], sm[:, 16 * LC + 15:16 * (LC + wid):16], num[:, 2:3], None, A.mult), ["sum%d" % t, "com%d" % t], ["tmp%d" % t])
+            do("v", lambda e: e.tensor_tensor(T.lists[:, lo:AL + TC], T.lists[:, lo:AL + TC], tmp[:, 0:wid], A.max), ["tmp%d" % t, "lista", "listb"], ["lista", "listb"])
+            do("v", lambda e: e.tensor_copy(lu[:, lo:AL + TC], T.lists[:, lo:AL + TC]), ["lista", "listb"], ["lu%d" % t])
+            tab = ("tc%d" % t, "ts%d" % t, 0, K) if t < R - 2 else ("ttc", "tts", 0, K)
+            for q, nm in (("v", "c"), ("a", "s")):
+                pick(q, tab, win, lu[:, AL:AL + TC], held(nm) + ["lu%d" % t], ["tab%s%d" % (nm, t)])
+            a, b = 128 * O * t, 128 * O * (t + 1)
+            do("v", lambda e: e.quantize_mx(T.wc[:, a:b], T.ws[:, a:b], T.wt[:, 4 * a:4 * b]), ["w"], ["wq%d" % t])
+            if t == R - 2:
+                c, d = 128 * O * n, 128 * O * (n + 1)
+                do("v", lambda e: e.quantize_mx(T.wc[:, c:d], T.ws[:, c:d], T.wt[:, 4 * c:4 * d]), ["w"], ["wq%d" % n])
+            quantise(k + 1)
+            if t < R - 2:
+                newer(n + 1)
+            else:
+                do("v", lambda e: e.tensor_tensor(T.fcf[:, :], T.lists[:, AL:AL + TC], T["sum%d" % n][:, 15:16 * TC:16], A.max), ["listb", "sum%d" % n], ["fcf"])
+                do("v", lambda e: e.tensor_copy(T.fcu[:, :], T.fcf[:, :]), ["fcf"], ["fcu"])
+        else:
+            tab = ("tc%d" % t, "ts%d" % t, 0, K)
+            for q, nm in (("v", "c"), ("a", "s")):
+                pick(q, tab, ("ttc", "tts", 0, 2 * K), pkl[:, :], ["tab%s%d" % (nm, t - 1), "wc%s%d" % (nm, n), "pk%d" % n], ["tab%s%d" % (nm, t)])
+        for o in range(O):
+            i = O * t + o
+            pb = 512 * (i % 4)
+            do("p", lambda e: e.matmul_mx(T.prod[:, pb:pb + K], T.wc[:, 128 * i:128 * i + 128], T.ws[:, 128 * i:128 * i + 128], T[tab[0]][:, 0:K], T[tab[1]][:, 0:K], True, True), ["wq%d" % t, "tabc%d" % t, "tabs%d" % t], ["prod%d" % (i % 4)])
+        for o in range(O):
+            i = O * t + o
+            pb = 512 * (i % 4)
+            y = slice(K * i, K * i + K)
+            if o % 2:
+                do("a", lambda e: e.activation(T.ty[:, y], T.prod[:, pb:pb + K], F.Copy), ["prod%d" % (i % 4)], ["ty%d" % i])
+            else:
+                do("v", lambda e: e.tensor_copy(T.ty[:, y], T.prod[:, pb:pb + K]), ["prod%d" % (i % 4)], ["ty%d" % i])
+            if t == R - 1:
+                q, sem = ("a", "yp") if o % 2 else ("s", "yo%d" % t)
+                dma(q, sem, T.y[:, y], T.ty[:, y], ["ty%d" % i], ["out%d" % i])
+        if t < R - 2:
+            m = n + 1
+            wn = ("pc%d" % (k + 1), "ps%d" % (k + 1), 0, end)
+            for q, nm in (("v", "c"), ("a", "s")):
+                pick(q, ("cc%d" % m, "cs_%d" % m, 0, NB), wn, T["lu%d" % t][:, LC * m:LC * m + LC], ["own%s%d" % (nm, k + 1), "cp%s%d" % (nm, k + 1), "lu%d" % t], ["nc%s%d" % (nm, m)])
+        if t + 2 < R:
+            later(t + 2)
+
+    hold("g", [(sem, None) for sem in sorted(total)])

@@ -1,4 +1,3 @@
-import numpy as np
 from concourse.bass import DstId, RemoteDMATransfer
 from concourse.mybir import dt, AluOpType, AxisListType, ActivationFunctionType
 
@@ -9,6 +8,7 @@ LC = NB // 16
 TC = K // 16
 AL = R * LC
 WIN = K + 16
+STEP = 128
 
 CODE, BYTE = "float8_e4m3fn_x4", "uint8"
 SCRATCH = {
@@ -30,9 +30,9 @@ SCRATCH = {
     "pp": ("sbuf", [128, 2], "int32"),
     "p16": ("sbuf", [128, 2], "int32"),
     "p16f": ("sbuf", [128, 2], "float32"),
-    "run": ("sbuf", [128, 640], "float32"),
+    "run": ("sbuf", [128, 384], "float32"),
     "mask": ("sbuf", [128, 384], "float32"),
-    "seg": ("sbuf", [128, 640], "float32"),
+    "seg": ("sbuf", [128, 384], "float32"),
     "jc": ("sbuf", [128, TC], "float32"),
     "jl": ("sbuf", [128, TC], "float32"),
     "vrow": ("sbuf", [128, NB], "float32"),
@@ -64,8 +64,8 @@ for _t in range(R):
     SCRATCH["tmp%d" % _t] = ("sbuf", [128, AL + TC], "float32")
     SCRATCH["lu%d" % _t] = ("sbuf", [128, AL + TC], "uint16")
     if _t:
-        SCRATCH["cc%d" % _t] = ("sbuf", [128, 2 * NB], CODE)
-        SCRATCH["cs_%d" % _t] = ("sbuf", [128, 2 * NB], BYTE)
+        SCRATCH["cc%d" % _t] = ("sbuf", [128, STEP + NB], CODE)
+        SCRATCH["cs_%d" % _t] = ("sbuf", [128, STEP + NB], BYTE)
         SCRATCH["ncf%d" % _t] = ("sbuf", [128, LC], "float32")
         SCRATCH["ncu%d" % _t] = ("sbuf", [128, LC], "uint16")
         SCRATCH["pk%d" % _t] = ("sbuf", [128, LC], "uint16")
@@ -73,12 +73,11 @@ for _t in range(R):
         SCRATCH["tc%d" % _t] = ("sbuf", [128, K], CODE)
         SCRATCH["ts%d" % _t] = ("sbuf", [128, K], BYTE)
 
-SEMAPHORES = ["vq", "aq", "pq", "gq", "snt", "lx0", "lx1", "lc0", "lc1", "ld0", "ld1", "lu", "lt", "lw0", "lw1"]
+SEMAPHORES = ["vq", "aq", "pq", "gq", "lx0", "lx1", "lc0", "lc1", "ld0", "ld1", "lu", "lt", "yp"]
 for _t in range(R):
-    SEMAPHORES += ["arrc%d" % _t, "arrs%d" % _t, "yo%d" % _t]
+    SEMAPHORES += ["arrc%d" % _t, "arrs%d" % _t, "yo%d" % _t, "snt%d" % _t, "lw%d" % _t]
 for _k in range(2, R + 1):
     SEMAPHORES += ["cp%d" % _k]
-SEMAPHORES += ["yp"]
 
 
 def deal(topo, cores, s):
@@ -169,6 +168,7 @@ def rank_program(g, core, T, topo):
             sem = "arr%s%d" % (nm, t)
             total[sem] = sum(ones(plans[s][h][r]) for s in range(N) if s != r)
             W["land%s%d" % (nm, t)] = [(sem, None)]
+        W["sent%d" % t] = [("snt%d" % t, None)]
 
     h = 2 * K
     dma("s", "lx0", T.xt[:, 0:h], T.x[:, 0:h], [], ["x"])
@@ -181,21 +181,26 @@ def rank_program(g, core, T, topo):
         q, n = ("s", "0") if i < 4 else ("a", "1")
         dma(q, "ld" + n, T.cdl[16 * i:16 * i + 16, :], T.cd[:, :], [], ["cd"])
     dma("s", "lt", T.thr1[0:1, :], T.thr[:, :], [], ["thr1"])
-    hw = 256 * R * O
-    dma("s", "lw0", T.wt[:, 0:hw], T.w[:, 0:hw], [], ["w"])
-    dma("s", "lw1", T.wt[:, hw:2 * hw], T.w[:, hw:2 * hw], [], ["w"])
 
-    do("v", lambda e: e.memset(T.inv[:, :], 0.0), [], ["inv%d" % t for t in range(R)])
-    do("v", lambda e: e.memset(T.zeros[:, :], 0), [], ["zeros"])
     fl = {"allow_small_or_imprecise_dtypes": True}
     do("g", lambda e: e.iota(T.pp[:, 0:1], [[0, 1]], 0, 1), [], ["pp"])
-    do("g", lambda e: e.iota(T.trash[:, :], [[0, R], [16, LC]], K + 1 - B * r, 0, **fl), [], ["trash"])
+    do("g", lambda e: e.iota(T.run[:, :], [[0, 24], [1, 16]], 0, 0, **fl), [], ["run"])
     do("g", lambda e: e.iota(T.jc[:, :], [[16, TC]], 0, 0, **fl), [], ["jc"])
+    do("g", lambda e: e.iota(T.trash[:, :], [[0, R], [16, LC]], K + 1 - B * r, 0, **fl), [], ["trash"])
     do("g", lambda e: e.iota(T.vrow[:, 0:B * (r + 1)], [[1, B * (r + 1)]], 0, 0, **fl), [], ["vrowa"])
     W["vrowb"] = []
     if r < N - 1:
         do("g", lambda e: e.iota(T.vrow[:, B * (r + 1):NB], [[1, NB - B * (r + 1)]], B * r, 0, **fl), [], ["vrowb"])
-    do("g", lambda e: e.iota(T.run[:, :], [[0, 40], [1, 16]], 0, 0, **fl), [], ["run"])
+    do("v", lambda e: e.memset(T.zeros[:, :], 0), [], ["zeros"])
+    for i in range(R):
+        do("v", lambda e: e.memset(T.inv[:, WIN * i:WIN * i + K], 0.0), [], ["inv%d" % i])
+    col = T.p16f[:, 0:1]
+    do("v", lambda e: e.tensor_scalar(T.p16[:, 0:1], T.pp[:, 0:1], 15, None, A.bitwise_and), ["pp"], ["p16"])
+    do("v", lambda e: e.tensor_copy(T.p16f[:, 0:1], T.p16[:, 0:1]), ["p16"], ["p16f"])
+    do("v", lambda e: e.tensor_scalar(T.mask[:, :], T.run[:, :], col, None, A.is_equal), ["run", "p16f"], ["mask"])
+    do("v", lambda e: e.tensor_scalar(T.jl[:, :], T.jc[:, :], col, None, A.add), ["jc", "p16f"], ["jl"])
+    do("v", lambda e: e.tensor_scalar(T.trash2[:, :], T.trash[:, :], col, None, A.add), ["trash", "p16f"], ["trash2"])
+    do("v", lambda e: e.tensor_copy(T.lists[:, AL:AL + TC], T.jl[:, :]), ["jl"], ["listb"])
 
     def quantise(k):
         do("v", lambda e: e.quantize_mx(T["pc%d" % k][:, 0:K], T["ps%d" % k][:, 0:K], T.xt[:, :]), ["x"], ["ownc%d" % k, "owns%d" % k])
@@ -219,34 +224,35 @@ def rank_program(g, core, T, topo):
                 if not scale:
                     src, dst = src.bitcast(dt.uint8), dst.bitcast(dt.uint8)
                 moves.append(RemoteDMATransfer(dst_ids=[DstId(rid=rid, pnc=pid)], dma_engine_mask=m[d], remote_sem=T.sem["arr%s%d" % (nm, t)], src=src, dst=dst))
-            g.remote_dma_fused(moves, local_sem=T.sem.snt)
-            total["snt"] = total.get("snt", 0) + sum(ones(m[d]) for d in m)
+            sem = "snt%d" % t
+            g.remote_dma_fused(moves, local_sem=T.sem[sem])
+            total[sem] = total.get(sem, 0) + sum(ones(m[d]) for d in m)
+
+    def fetch(t):
+        a, b = 512 * O * t, 512 * O * (t + 1)
+        dma("s", "lw%d" % t, T.wt[:, a:b], T.w[:, a:b], ["sent%d" % max(t - 1, 0)], ["w%d" % t])
 
     quantise(0)
     do("v", lambda e: e.tensor_copy(T.csu[:, :], T.csl[:, :]), ["cs"], ["csu"])
     pick("v", ("sc0", "ss0", 0, NB), ("pc0", "ps0", 0, K), T.csu[:, 0:LC], ["ownc0", "csu"], ["sndc0"])
     pick("a", ("sc0", "ss0", 0, NB), ("pc0", "ps0", 0, K), T.csu[:, 0:LC], ["owns0", "csu"], ["snds0"])
     send(0)
+    fetch(0)
+    fetch(1)
     do("g", lambda e: e.partition_broadcast(T.thri[:, :], T.thr1[0:1, :], 128), ["thr1"], ["thri"])
 
     quantise(1)
     do("v", lambda e: e.quantize_mx(T.uc[:, :], T.us[:, :], T.ut[:, :]), ["u"], ["uc", "us"])
+    do("v", lambda e: e.tensor_scalar(T.own1[:, :], T.cdl[:, :], 0.0, None, A.is_lt), ["cd"], ["own1"])
     pick("v", ("vc", "vs", 0, 128), ("uc", "us", 0, 128), T.zeros[:, :], ["uc", "zeros"], ["vc"])
     pick("a", ("vc", "vs", 0, 128), ("uc", "us", 0, 128), T.zeros[:, :], ["us", "zeros"], ["vs"])
+    do("v", lambda e: e.tensor_tensor(T.own2[:, :], T.own1[:, :], T.trash2[:, :], A.mult), ["own1", "trash2"], ["own2"])
     pick("v", ("cc1", "cs_1", 0, NB), ("pc1", "ps1", 0, K), T.csu[:, LC:2 * LC], ["ownc1", "csu"], ["ncc1"])
     pick("a", ("cc1", "cs_1", 0, NB), ("pc1", "ps1", 0, K), T.csu[:, LC:2 * LC], ["owns1", "csu"], ["ncs1"])
-    do("v", lambda e: e.tensor_scalar(T.p16[:, 0:1], T.pp[:, 0:1], 15, None, A.bitwise_and), ["pp"], ["p16"])
-    do("v", lambda e: e.tensor_scalar(T.own1[:, :], T.cdl[:, :], 0.0, None, A.is_lt), ["cd"], ["own1"])
-    do("v", lambda e: e.tensor_copy(T.p16f[:, 0:1], T.p16[:, 0:1]), ["p16"], ["p16f"])
-    do("v", lambda e: e.tensor_scalar(T.lists[:, 0:AL], T.csl[:, :], 0.0, None, A.max), ["cs"], ["lista"])
-    col = T.p16f[:, 0:1]
-    do("v", lambda e: e.tensor_scalar(T.trash2[:, :], T.trash[:, :], col, None, A.add), ["trash", "p16f"], ["trash2"])
-    do("v", lambda e: e.tensor_scalar(T.jl[:, :], T.jc[:, :], col, None, A.add), ["jc", "p16f"], ["jl"])
-    do("v", lambda e: e.tensor_tensor(T.own2[:, :], T.own1[:, :], T.trash2[:, :], A.mult), ["own1", "trash2"], ["own2"])
-    do("v", lambda e: e.tensor_scalar(T.mask[:, :], T.run[:, 0:384], col, None, A.is_equal), ["run", "p16f"], ["mask"])
     do("v", lambda e: e.tensor_tensor(T.cdf[:, :], T.cdl[:, :], T.own2[:, :], A.add), ["cd", "own2"], ["cdf"])
-    do("v", lambda e: e.tensor_scalar(T.val0[:, :], T.vrow[:, :], float(K), None, A.add), ["vrowa", "vrowb"], ["val0"])
+    do("v", lambda e: e.tensor_scalar(T.lists[:, 0:AL], T.csl[:, :], 0.0, None, A.max), ["cs"], ["lista"])
     do("v", lambda e: e.tensor_copy(T.cdo[:, :], T.cdf[:, :]), ["cdf"], ["cdo"])
+    do("v", lambda e: e.tensor_scalar(T.val0[:, :], T.vrow[:, :], float(K), None, A.add), ["vrowa", "vrowb"], ["val0"])
     do("v", lambda e: e.tensor_scalar(T.seg[:, :], T.run[:, :], 0.5, None, A.is_gt), ["run"], ["seg"])
 
     def later(t):
@@ -256,28 +262,23 @@ def rank_program(g, core, T, topo):
             do("v", lambda e: e.tensor_scalar(T[v][:, :], T.vrow[:, :], float(K + NEW * t), None, A.add), ["vrowa", "vrowb"], [v])
         do("v", lambda e: e.tensor_copy(T.inv[:, a:a + WIN].indirect(T.cdo[:, LC * t:LC * t + LC]), T[v][:, :]), [v, "cdo"], ["inv%d" % t])
         if n:
-            do("v", lambda e: e.tensor_tensor(T[l][:, 0:n], T.inv[:, a:a + WIN].indirect(T.csu[:, LC * (t + 1):AL]), T.mask[:, 0:n], A.mult), ["inv%d" % t, "csu", "mask"], [l + "a"])
-        else:
-            W[l + "a"] = []
+            do("v", lambda e: e.tensor_tensor(T[l][:, 0:n], T.inv[:, a:a + K].indirect(T.csu[:, LC * (t + 1):AL]), T.mask[:, 0:n], A.mult), ["inv%d" % t, "csu", "mask"], [l + "a"])
+            do("v", lambda e: e.tensor_tensor_scan(T[s][:, 0:n], T.seg[:, 0:n], T[l][:, 0:n], 0.0, A.mult, A.add), ["seg", l + "a"], [s + "a"])
         do("v", lambda e: e.tensor_tensor(T[l][:, n:n + K], T.inv[:, a:a + K], T.mask[:, 0:K], A.mult), ["inv%d" % t, "mask"], [l + "b"])
-        do("v", lambda e: e.tensor_tensor_scan(T[s][:, 0:n + K], T.seg[:, 0:n + K], T[l][:, 0:n + K], 0.0, A.mult, A.add), ["seg", l + "a", l + "b"], [s])
+        do("v", lambda e: e.tensor_tensor_scan(T[s][:, n:n + K], T.seg[:, 0:K], T[l][:, n:n + K], 0.0, A.mult, A.add), ["seg", l + "b"], [s + "b"])
 
     def newer(t):
-        do("v", lambda e: e.tensor_tensor(T["ncf%d" % t][:, :], T.lists[:, LC * t:LC * t + LC], T["sum%d" % (t - 1)][:, 15:16 * LC:16], A.max), ["lista", "sum%d" % (t - 1)], ["ncf%d" % t])
+        do("v", lambda e: e.tensor_tensor(T["ncf%d" % t][:, :], T.lists[:, LC * t:LC * t + LC], T["sum%d" % (t - 1)][:, 15:16 * LC:16], A.max), ["lista", "sum%da" % (t - 1)], ["ncf%d" % t])
         do("v", lambda e: e.tensor_copy(T["ncu%d" % t][:, :], T["ncf%d" % t][:, :]), ["ncf%d" % t], ["ncu%d" % t])
 
     later(0)
     newer(1)
-    do("v", lambda e: e.tensor_copy(T.lists[:, AL:AL + TC], T.jl[:, :]), ["jl"], ["listb"])
     do("v", lambda e: e.tensor_copy(T.thrf[:, :], T.thri[:, :]), ["thri"], ["thrf"])
-    later(1)
 
     for t in range(R):
-        k, n = t + 1, t + 1
+        k = n = t + 1
         end = K + NEW * k
-        base = end - NEW
         num, bit = T["num%d" % t], "bit%d" % t
-        rest = ["c%d" % k] if t else []
         held = lambda x: ["own%s%d" % (x, k), "land%s%d" % (x, t)] + (["cp%s%d" % (x, k)] if t else [])
         if t < R - 1:
             for nm in ("c", "s"):
@@ -285,75 +286,80 @@ def rank_program(g, core, T, topo):
                 if nm == "c":
                     o, i = o.bitcast(dt.uint8), i.bitcast(dt.uint8)
                 dma("s", "cp%d" % (k + 1), o, i, ["land%s%d" % (nm, t)] + (["cp%s%d" % (nm, k)] if t else []), ["cp%s%d" % (nm, k + 1)])
-        if t:
-            y = slice(O * K * (t - 1), O * K * t)
-            dma("s", "yo%d" % (t - 1), T.y[:, y], T.ty[:, y], ["landc%d" % t, "ty%d" % (O * (t - 1)), "ty%d" % (O * (t - 1) + 1)], ["out%d" % (t - 1)])
         sb = 512 * (t % 2)
         do("p", lambda e: e.matmul_mx(T.acc[:, sb:sb + 128], T.vc[:, :], T.vs[:, :], T["pc%d" % k][:, end - 128:end], T["ps%d" % k][:, end - 128:end], True, True), ["vc", "vs"] + held("c") + held("s"), ["acc%d" % (t % 2)])
         if t < R - 1:
-            out, off, ck, cv = ("cc%d" % n, "cs_%d" % n, NB, 2 * NB), T["ncu%d" % n][:, :], "wc%s%d", "ncu%d" % n
+            out, off, cv = ("cc%d" % n, "cs_%d" % n, STEP, STEP + NB), T["ncu%d" % n][:, :], "ncu%d" % n
         else:
-            out, off, ck, cv = ("ttc", "tts", K, 2 * K), T.fcu[:, :], "wc%s%d", "fcu"
+            out, off, cv = ("ttc", "tts", K, 2 * K), T.fcu[:, :], "fcu"
         win = ("pc%d" % k, "ps%d" % k, 0, end)
-        pick("v", out, win, off, held("c") + [cv], [ck % ("c", n)])
-        pick("a", out, win, off, held("s") + [cv], [ck % ("s", n)])
+        for q, nm in (("v", "c"), ("a", "s")):
+            pick(q, out, win, off, held(nm) + [cv], ["wc%s%d" % (nm, n)])
         do("v", lambda e: e.tensor_scalar(T[bit][:, :], T.acc[:, sb + 128 - NEW:sb + 128], 0.0, None, A.is_ge), ["acc%d" % (t % 2)], [bit])
         do("v", lambda e: e.tensor_reduce(num[:, 0:1], T[bit][:, :], AxisListType.X, A.add), [bit], ["cnt%d" % t])
-        step, width = (NB, LC) if t < R - 1 else (K, TC)
+        step, width = (STEP, LC) if t < R - 1 else (K, TC)
         do("v", lambda e: e.tensor_scalar(num[:, 1:2], num[:, 0:1], T.thrf[:, t:t + 1], float(step), A.is_ge, A.mult), ["cnt%d" % t, "thrf"], ["shift%d" % t])
         pkl = T["pk%d" % n] if t < R - 1 else T.pkl
         do("v", lambda e: e.tensor_scalar(pkl[:, :], T.jl[:, 0:width], num[:, 1:2], None, A.add), ["jl", "shift%d" % t], ["pk%d" % n])
         if t < R - 1:
-            src, dst = ("cc%d" % n, "cs_%d" % n, 0, 2 * NB), ("sc%d" % n, "ss%d" % n, 0, NB)
+            src, dst = ("cc%d" % n, "cs_%d" % n, 0, STEP + NB), ("sc%d" % n, "ss%d" % n, 0, NB)
             for q, nm in (("v", "c"), ("a", "s")):
                 pick(q, dst, src, pkl[:, :], ["nc%s%d" % (nm, n), "wc%s%d" % (nm, n), "pk%d" % n], ["snd%s%d" % (nm, n)])
             send(n)
-            do("v", lambda e: e.tensor_scalar(num[:, 2:3], num[:, 0:1], T.thrf[:, t:t + 1], None, A.is_ge), ["cnt%d" % t, "thrf"], ["com%d" % t])
             lo = LC * (t + 2)
             wid = AL + TC - lo
             tmp, lu, sm = T["tmp%d" % t], T["lu%d" % t], T["sum%d" % t]
-            do("v", lambda e: e.tensor_scalar(tmp[:, 0:wid], sm[:, 16 * LC + 15:16 * (LC + wid):16], num[:, 2:3], None, A.mult), ["sum%d" % t, "com%d" % t], ["tmp%d" % t])
+            do("v", lambda e: e.tensor_scalar(tmp[:, 0:wid], sm[:, 16 * LC + 15:16 * (LC + wid):16], num[:, 1:2], 1.0 / STEP, A.mult, A.mult), ["sum%da" % t, "sum%db" % t, "shift%d" % t], ["tmp%d" % t])
             do("v", lambda e: e.tensor_tensor(T.lists[:, lo:AL + TC], T.lists[:, lo:AL + TC], tmp[:, 0:wid], A.max), ["tmp%d" % t, "lista", "listb"], ["lista", "listb"])
             do("v", lambda e: e.tensor_copy(lu[:, lo:AL + TC], T.lists[:, lo:AL + TC]), ["lista", "listb"], ["lu%d" % t])
             tab = ("tc%d" % t, "ts%d" % t, 0, K) if t < R - 2 else ("ttc", "tts", 0, K)
             for q, nm in (("v", "c"), ("a", "s")):
                 pick(q, tab, win, lu[:, AL:AL + TC], held(nm) + ["lu%d" % t], ["tab%s%d" % (nm, t)])
-            a, b = 128 * O * t, 128 * O * (t + 1)
-            do("v", lambda e: e.quantize_mx(T.wc[:, a:b], T.ws[:, a:b], T.wt[:, 4 * a:4 * b]), ["w"], ["wq%d" % t])
-            if t == R - 2:
-                c, d = 128 * O * n, 128 * O * (n + 1)
-                do("v", lambda e: e.quantize_mx(T.wc[:, c:d], T.ws[:, c:d], T.wt[:, 4 * c:4 * d]), ["w"], ["wq%d" % n])
+            for i in [t] + ([n] if t == R - 2 else []):
+                a, b = 128 * O * i, 128 * O * (i + 1)
+                do("v", lambda e: e.quantize_mx(T.wc[:, a:b], T.ws[:, a:b], T.wt[:, 4 * a:4 * b]), ["w%d" % i], ["wq%d" % i])
+            for o in range(O):
+                i = O * t + o
+                pb = 512 * (i % 4)
+                do("p", lambda e: e.matmul_mx(T.prod[:, pb:pb + K], T.wc[:, 128 * i:128 * i + 128], T.ws[:, 128 * i:128 * i + 128], T[tab[0]][:, 0:K], T[tab[1]][:, 0:K], True, True), ["wq%d" % t, "tabc%d" % t, "tabs%d" % t], ["prod%d" % (i % 4)])
+            for o in range(O):
+                i = O * t + o
+                pb = 512 * (i % 4)
+                do("a", lambda e: e.activation(T.ty[:, K * i:K * i + K], T.prod[:, pb:pb + K], F.Copy), ["prod%d" % (i % 4)], ["ty%d" % i])
+            if n + 1 < R:
+                fetch(n + 1)
+            y = slice(O * K * t, O * K * (t + 1))
+            dma("s", "yo%d" % t, T.y[:, y], T.ty[:, y], ["sent%d" % n, "ty%d" % (O * t), "ty%d" % (O * t + 1)], ["out%d" % t])
+            later(n)
             quantise(k + 1)
             if t < R - 2:
                 newer(n + 1)
+                m = n + 1
+                wn = ("pc%d" % (k + 1), "ps%d" % (k + 1), 0, end)
+                for q, nm in (("v", "c"), ("a", "s")):
+                    pick(q, ("cc%d" % m, "cs_%d" % m, 0, NB), wn, lu[:, LC * m:LC * m + LC], ["own%s%d" % (nm, k + 1), "cp%s%d" % (nm, k + 1), "lu%d" % t], ["nc%s%d" % (nm, m)])
             else:
-                do("v", lambda e: e.tensor_tensor(T.fcf[:, :], T.lists[:, AL:AL + TC], T["sum%d" % n][:, 15:16 * TC:16], A.max), ["listb", "sum%d" % n], ["fcf"])
+                do("v", lambda e: e.tensor_tensor(T.fcf[:, :], T.lists[:, AL:AL + TC], T["sum%d" % n][:, 15:16 * TC:16], A.max), ["listb", "sum%db" % n], ["fcf"])
                 do("v", lambda e: e.tensor_copy(T.fcu[:, :], T.fcf[:, :]), ["fcf"], ["fcu"])
         else:
-            tab = ("tc%d" % t, "ts%d" % t, 0, K)
-            for q, nm in (("v", "c"), ("a", "s")):
-                pick(q, tab, ("ttc", "tts", 0, 2 * K), pkl[:, :], ["tab%s%d" % (nm, t - 1), "wc%s%d" % (nm, n), "pk%d" % n], ["tab%s%d" % (nm, t)])
-        for o in range(O):
-            i = O * t + o
-            pb = 512 * (i % 4)
-            do("p", lambda e: e.matmul_mx(T.prod[:, pb:pb + K], T.wc[:, 128 * i:128 * i + 128], T.ws[:, 128 * i:128 * i + 128], T[tab[0]][:, 0:K], T[tab[1]][:, 0:K], True, True), ["wq%d" % t, "tabc%d" % t, "tabs%d" % t], ["prod%d" % (i % 4)])
-        for o in range(O):
-            i = O * t + o
-            pb = 512 * (i % 4)
-            y = slice(K * i, K * i + K)
-            if o % 2:
-                do("a", lambda e: e.activation(T.ty[:, y], T.prod[:, pb:pb + K], F.Copy), ["prod%d" % (i % 4)], ["ty%d" % i])
-            else:
-                do("v", lambda e: e.tensor_copy(T.ty[:, y], T.prod[:, pb:pb + K]), ["prod%d" % (i % 4)], ["ty%d" % i])
-            if t == R - 1:
-                q, sem = ("a", "yp") if o % 2 else ("s", "yo%d" % t)
-                dma(q, sem, T.y[:, y], T.ty[:, y], ["ty%d" % i], ["out%d" % i])
-        if t < R - 2:
-            m = n + 1
-            wn = ("pc%d" % (k + 1), "ps%d" % (k + 1), 0, end)
-            for q, nm in (("v", "c"), ("a", "s")):
-                pick(q, ("cc%d" % m, "cs_%d" % m, 0, NB), wn, T["lu%d" % t][:, LC * m:LC * m + LC], ["own%s%d" % (nm, k + 1), "cp%s%d" % (nm, k + 1), "lu%d" % t], ["nc%s%d" % (nm, m)])
-        if t + 2 < R:
-            later(t + 2)
+            H = K // 2
+            for h in range(2):
+                tab = ("tc%d" % t, "ts%d" % t, H * h, H * h + H)
+                for q, nm in (("v", "c"), ("a", "s")):
+                    pick(q, tab, ("ttc", "tts", 0, 2 * K), pkl[:, TC // 2 * h:TC // 2 * (h + 1)], ["tab%s%d" % (nm, t - 1), "wc%s%d" % (nm, n), "pk%d" % n], ["tab%s%d%d" % (nm, t, h)])
+                for o in range(O):
+                    i = O * t + o
+                    pb = 512 * (2 * h + o)
+                    do("p", lambda e: e.matmul_mx(T.prod[:, pb:pb + H], T.wc[:, 128 * i:128 * i + 128], T.ws[:, 128 * i:128 * i + 128], T[tab[0]][:, tab[2]:tab[3]], T[tab[1]][:, tab[2]:tab[3]], True, True), ["wq%d" % t, "tabc%d%d" % (t, h), "tabs%d%d" % (t, h)], ["prod%d" % (2 * h + o)])
+            for h in range(2):
+                for o in range(O):
+                    a, pb = K * (O * t + o) + H * h, 512 * (2 * h + o)
+                    y = slice(a, a + H)
+                    if o:
+                        do("a", lambda e: e.activation(T.ty[:, y], T.prod[:, pb:pb + H], F.Copy), ["prod%d" % (2 * h + o)], ["tyz%d%d" % (h, o)])
+                    else:
+                        do("v", lambda e: e.tensor_copy(T.ty[:, y], T.prod[:, pb:pb + H]), ["prod%d" % (2 * h + o)], ["tyz%d%d" % (h, o)])
+                    q, sem = ("a", "yp") if o and h else ("s", "yo%d" % t)
+                    dma(q, sem, T.y[:, y], T.ty[:, y], ["tyz%d%d" % (h, o)], ["outz%d%d" % (h, o)])
 
     hold("g", [(sem, None) for sem in sorted(total)])

@@ -1,5 +1,5 @@
 from concourse.bass import DstId, RemoteDMATransfer
-from concourse.mybir import dt, AluOpType, AxisListType, ActivationFunctionType
+from concourse.mybir import dt, AluOpType, ActivationFunctionType
 
 N, K, B, R, O = 8, 256, 12, 5, 2
 NB = N * B
@@ -9,6 +9,7 @@ TC = K // 16
 AL = R * LC
 WIN = K + 16
 STEP = 128
+TINY = 1e-30
 
 CODE, BYTE = "float8_e4m3fn_x4", "uint8"
 SCRATCH = {
@@ -60,7 +61,7 @@ for _t in range(R):
     SCRATCH["lin%d" % _t] = ("sbuf", [128, 640], "float32")
     SCRATCH["sum%d" % _t] = ("sbuf", [128, 640], "float32")
     SCRATCH["bit%d" % _t] = ("sbuf", [128, NEW], "bfloat16")
-    SCRATCH["num%d" % _t] = ("sbuf", [128, 4], "float32")
+    SCRATCH["num%d" % _t] = ("sbuf", [128, 8], "float32")
     SCRATCH["tmp%d" % _t] = ("sbuf", [128, AL + TC], "float32")
     SCRATCH["lu%d" % _t] = ("sbuf", [128, AL + TC], "uint16")
     if _t:
@@ -78,6 +79,8 @@ for _t in range(R):
     SEMAPHORES += ["arrc%d" % _t, "arrs%d" % _t, "yo%d" % _t, "snt%d" % _t, "lw%d" % _t]
 for _k in range(2, R + 1):
     SEMAPHORES += ["cp%d" % _k]
+for _k in range(3, R + 1):
+    SEMAPHORES += ["co%d" % _k]
 
 
 def deal(topo, cores, s):
@@ -87,21 +90,17 @@ def deal(topo, cores, s):
         if d != s:
             (home if topo.chip(cores[d]) == topo.chip(src) else off).append(d)
     near = lambda d: topo.mates(topo.chip(src), topo.chip(cores[d])) or topo.same_plane(topo.chip(src), topo.chip(cores[d]))
-    off = [d for d in off if not near(d)] + [d for d in off if near(d)]
     eng = topo.engines(src, cores[off[0]])
+    even, odd = eng[0::2], eng[1::2]
     two = len(eng) - len(off)
-    half = 2 * two
+    off = [d for d in off if not near(d)] + [d for d in off if near(d)]
     codes, scales = {}, {}
     for i, d in enumerate(off):
-        codes[d] = [eng[2 * i], eng[2 * i + 1]] if i < two else [eng[half + i - two]]
-    one = off[two:] + off[:two]
-    for i, d in enumerate(one):
-        k = len(off) - two
-        scales[d] = [eng[i]] if i < k else [eng[k + 2 * (i - k)], eng[k + 2 * (i - k) + 1]]
+        codes[d] = even[2 * i:2 * i + 2] if i < two else [odd[i - two]]
+        scales[d] = odd[2 * i:2 * i + 2] if i < two else [even[i - two]]
     for d in home:
         rest = [e for e in topo.engines(src, cores[d]) if e not in eng]
-        pick = rest[::max(1, len(rest) // 2)][:2]
-        codes[d], scales[d] = pick, pick
+        codes[d] = scales[d] = rest[::max(1, len(rest) // 2)][:2]
     bits = lambda m: {d: sum(1 << e for e in m[d]) for d in m}
     return bits(codes), bits(scales)
 
@@ -205,9 +204,11 @@ def rank_program(g, core, T, topo):
     def quantise(k):
         do("v", lambda e: e.quantize_mx(T["pc%d" % k][:, 0:K], T["ps%d" % k][:, 0:K], T.xt[:, :]), ["x"], ["ownc%d" % k, "owns%d" % k])
 
-    def pick(q, out, win, off, rd, wr):
-        if q == "v":
+    def pick(q, nm, out, win, off, rd, wr):
+        if nm == "c":
             do("v", lambda e: e.tensor_copy(T[out[0]][:, out[2]:out[3]].bitcast(dt.uint32), T[win[0]][:, win[2]:win[3]].bitcast(dt.uint32).indirect(off)), rd, wr)
+        elif q == "v":
+            do("v", lambda e: e.tensor_copy(T[out[1]][:, out[2]:out[3]], T[win[1]][:, win[2]:win[3]].indirect(off)), rd, wr)
         else:
             do("a", lambda e: e.activation(T[out[1]][:, out[2]:out[3]], T[win[1]][:, win[2]:win[3]].indirect(off), F.Copy), rd, wr)
 
@@ -232,60 +233,71 @@ def rank_program(g, core, T, topo):
         a, b = 512 * O * t, 512 * O * (t + 1)
         dma("s", "lw%d" % t, T.wt[:, a:b], T.w[:, a:b], ["sent%d" % max(t - 1, 0)], ["w%d" % t])
 
+    def carry(name, k, a, b, rd):
+        for nm in ("c", "s"):
+            o, i = T["p%s%d" % (nm, k)][:, a:b], T["p%s%d" % (nm, k - 1)][:, a:b]
+            if nm == "c":
+                o, i = o.bitcast(dt.uint8), i.bitcast(dt.uint8)
+            dma("s", "%s%d" % (name, k), o, i, rd(nm), ["%s%s%d" % (name, nm, k)])
+
     quantise(0)
     do("v", lambda e: e.tensor_copy(T.csu[:, :], T.csl[:, :]), ["cs"], ["csu"])
-    pick("v", ("sc0", "ss0", 0, NB), ("pc0", "ps0", 0, K), T.csu[:, 0:LC], ["ownc0", "csu"], ["sndc0"])
-    pick("a", ("sc0", "ss0", 0, NB), ("pc0", "ps0", 0, K), T.csu[:, 0:LC], ["owns0", "csu"], ["snds0"])
+    for nm in ("c", "s"):
+        pick("a", nm, ("sc0", "ss0", 0, NB), ("pc0", "ps0", 0, K), T.csu[:, 0:LC], ["own%s0" % nm, "csu"], ["snd%s0" % nm])
     send(0)
     fetch(0)
     fetch(1)
     do("g", lambda e: e.partition_broadcast(T.thri[:, :], T.thr1[0:1, :], 128), ["thr1"], ["thri"])
 
-    quantise(1)
-    do("v", lambda e: e.quantize_mx(T.uc[:, :], T.us[:, :], T.ut[:, :]), ["u"], ["uc", "us"])
-    do("v", lambda e: e.tensor_scalar(T.own1[:, :], T.cdl[:, :], 0.0, None, A.is_lt), ["cd"], ["own1"])
-    pick("v", ("vc", "vs", 0, 128), ("uc", "us", 0, 128), T.zeros[:, :], ["uc", "zeros"], ["vc"])
-    pick("a", ("vc", "vs", 0, 128), ("uc", "us", 0, 128), T.zeros[:, :], ["us", "zeros"], ["vs"])
-    do("v", lambda e: e.tensor_tensor(T.own2[:, :], T.own1[:, :], T.trash2[:, :], A.mult), ["own1", "trash2"], ["own2"])
-    pick("v", ("cc1", "cs_1", 0, NB), ("pc1", "ps1", 0, K), T.csu[:, LC:2 * LC], ["ownc1", "csu"], ["ncc1"])
-    pick("a", ("cc1", "cs_1", 0, NB), ("pc1", "ps1", 0, K), T.csu[:, LC:2 * LC], ["owns1", "csu"], ["ncs1"])
-    do("v", lambda e: e.tensor_tensor(T.cdf[:, :], T.cdl[:, :], T.own2[:, :], A.add), ["cd", "own2"], ["cdf"])
-    do("v", lambda e: e.tensor_scalar(T.lists[:, 0:AL], T.csl[:, :], 0.0, None, A.max), ["cs"], ["lista"])
-    do("v", lambda e: e.tensor_copy(T.cdo[:, :], T.cdf[:, :]), ["cdf"], ["cdo"])
-    do("v", lambda e: e.tensor_scalar(T.val0[:, :], T.vrow[:, :], float(K), None, A.add), ["vrowa", "vrowb"], ["val0"])
-    do("v", lambda e: e.tensor_scalar(T.seg[:, :], T.run[:, :], 0.5, None, A.is_gt), ["run"], ["seg"])
-
     def later(t):
         v, s, l, a = "val%d" % t, "sum%d" % t, "lin%d" % t, WIN * t
         n = NB * (R - 1 - t)
-        if t:
-            do("v", lambda e: e.tensor_scalar(T[v][:, :], T.vrow[:, :], float(K + NEW * t), None, A.add), ["vrowa", "vrowb"], [v])
+        do("v", lambda e: e.tensor_scalar(T[v][:, :], T.vrow[:, :], float(K + NEW * t), None, A.add), ["vrowa", "vrowb"], [v])
+        yield
         do("v", lambda e: e.tensor_copy(T.inv[:, a:a + WIN].indirect(T.cdo[:, LC * t:LC * t + LC]), T[v][:, :]), [v, "cdo"], ["inv%d" % t])
+        yield
         if n:
             do("v", lambda e: e.tensor_tensor(T[l][:, 0:n], T.inv[:, a:a + K].indirect(T.csu[:, LC * (t + 1):AL]), T.mask[:, 0:n], A.mult), ["inv%d" % t, "csu", "mask"], [l + "a"])
-            do("v", lambda e: e.tensor_tensor_scan(T[s][:, 0:n], T.seg[:, 0:n], T[l][:, 0:n], 0.0, A.mult, A.add), ["seg", l + "a"], [s + "a"])
         do("v", lambda e: e.tensor_tensor(T[l][:, n:n + K], T.inv[:, a:a + K], T.mask[:, 0:K], A.mult), ["inv%d" % t, "mask"], [l + "b"])
+        if n:
+            do("v", lambda e: e.tensor_tensor_scan(T[s][:, 0:n], T.seg[:, 0:n], T[l][:, 0:n], 0.0, A.mult, A.add), ["seg", l + "a"], [s + "a"])
         do("v", lambda e: e.tensor_tensor_scan(T[s][:, n:n + K], T.seg[:, 0:K], T[l][:, n:n + K], 0.0, A.mult, A.add), ["seg", l + "b"], [s + "b"])
+        yield
 
     def newer(t):
         do("v", lambda e: e.tensor_tensor(T["ncf%d" % t][:, :], T.lists[:, LC * t:LC * t + LC], T["sum%d" % (t - 1)][:, 15:16 * LC:16], A.max), ["lista", "sum%da" % (t - 1)], ["ncf%d" % t])
+        yield
         do("v", lambda e: e.tensor_copy(T["ncu%d" % t][:, :], T["ncf%d" % t][:, :]), ["ncf%d" % t], ["ncu%d" % t])
+        yield
 
-    later(0)
-    newer(1)
-    do("v", lambda e: e.tensor_copy(T.thrf[:, :], T.thri[:, :]), ["thri"], ["thrf"])
+    w0, n1 = later(0), newer(1)
+    quantise(1)
+    do("v", lambda e: e.tensor_scalar(T.own1[:, :], T.cdl[:, :], 0.0, None, A.is_lt), ["cd"], ["own1"])
+    do("v", lambda e: e.quantize_mx(T.uc[:, :], T.us[:, :], T.ut[:, :]), ["u"], ["uc", "us"])
+    do("v", lambda e: e.tensor_tensor(T.own2[:, :], T.own1[:, :], T.trash2[:, :], A.mult), ["own1", "trash2"], ["own2"])
+    for nm in ("c", "s"):
+        pick("a", nm, ("vc", "vs", 0, 128), ("uc", "us", 0, 128), T.zeros[:, :], ["u" + nm, "zeros"], ["v" + nm])
+    do("v", lambda e: e.tensor_tensor(T.cdf[:, :], T.cdl[:, :], T.own2[:, :], A.add), ["cd", "own2"], ["cdf"])
+    for nm in ("c", "s"):
+        pick("a", nm, ("cc1", "cs_1", 0, NB), ("pc1", "ps1", 0, K), T.csu[:, LC:2 * LC], ["own%s1" % nm, "csu"], ["nc%s1" % nm])
+    do("v", lambda e: e.tensor_copy(T.cdo[:, :], T.cdf[:, :]), ["cdf"], ["cdo"])
+    next(w0)
+    do("v", lambda e: e.tensor_scalar(T.lists[:, 0:AL], T.csl[:, :], 0.0, None, A.max), ["cs"], ["lista"])
+    next(w0)
+    do("v", lambda e: e.tensor_scalar(T.seg[:, :], T.run[:, :], 0.5, None, A.is_gt), ["run"], ["seg"])
+    next(w0)
+    next(n1)
+    do("v", lambda e: e.tensor_scalar(T.thrf[:, :], T.thri[:, :], 2.0, float(-NEW), A.mult, A.add), ["thri"], ["thrf"])
+    next(n1)
 
     for t in range(R):
         k = n = t + 1
         end = K + NEW * k
-        num, bit = T["num%d" % t], "bit%d" % t
-        held = lambda x: ["own%s%d" % (x, k), "land%s%d" % (x, t)] + (["cp%s%d" % (x, k)] if t else [])
+        num, bit = T["num%d" % t], T["bit%d" % t]
+        past = lambda x, j: (["cp%s%d" % (x, j)] if j > 1 else []) + (["co%s%d" % (x, j)] if j > 2 else [])
+        held = lambda x: ["own%s%d" % (x, k), "land%s%d" % (x, t)] + past(x, k)
         if t < R - 1:
-            for nm in ("c", "s"):
-                o, i = T["p%s%d" % (nm, k + 1)][:, K:end], T["p%s%d" % (nm, k)][:, K:end]
-                if nm == "c":
-                    o, i = o.bitcast(dt.uint8), i.bitcast(dt.uint8)
-                dma("s", "cp%d" % (k + 1), o, i, ["land%s%d" % (nm, t)] + (["cp%s%d" % (nm, k)] if t else []), ["cp%s%d" % (nm, k + 1)])
+            carry("cp", k + 1, end - NEW, end, lambda x: ["land%s%d" % (x, t)])
         sb = 512 * (t % 2)
         do("p", lambda e: e.matmul_mx(T.acc[:, sb:sb + 128], T.vc[:, :], T.vs[:, :], T["pc%d" % k][:, end - 128:end], T["ps%d" % k][:, end - 128:end], True, True), ["vc", "vs"] + held("c") + held("s"), ["acc%d" % (t % 2)])
         if t < R - 1:
@@ -293,31 +305,33 @@ def rank_program(g, core, T, topo):
         else:
             out, off, cv = ("ttc", "tts", K, 2 * K), T.fcu[:, :], "fcu"
         win = ("pc%d" % k, "ps%d" % k, 0, end)
-        for q, nm in (("v", "c"), ("a", "s")):
-            pick(q, out, win, off, held(nm) + [cv], ["wc%s%d" % (nm, n)])
-        do("v", lambda e: e.tensor_scalar(T[bit][:, :], T.acc[:, sb + 128 - NEW:sb + 128], 0.0, None, A.is_ge), ["acc%d" % (t % 2)], [bit])
-        do("v", lambda e: e.tensor_reduce(num[:, 0:1], T[bit][:, :], AxisListType.X, A.add), [bit], ["cnt%d" % t])
+        for nm in ("c", "s"):
+            pick("v", nm, out, win, off, held(nm) + [cv], ["wc%s%d" % (nm, n)])
+        do("a", lambda e: e.activation(bit[:, :], T.acc[:, sb + 128 - NEW:sb + 128], F.Sign, bias=TINY, accum_out=num[:, 0:1]), ["acc%d" % (t % 2)], ["cnt%d" % t])
         step, width = (STEP, LC) if t < R - 1 else (K, TC)
-        do("v", lambda e: e.tensor_scalar(num[:, 1:2], num[:, 0:1], T.thrf[:, t:t + 1], float(step), A.is_ge, A.mult), ["cnt%d" % t, "thrf"], ["shift%d" % t])
+        do("v", lambda e: e.tensor_scalar(num[:, 4:5], num[:, 0:1], T.thrf[:, t:t + 1], float(step), A.is_ge, A.mult), ["cnt%d" % t, "thrf"], ["shift%d" % t])
         pkl = T["pk%d" % n] if t < R - 1 else T.pkl
-        do("v", lambda e: e.tensor_scalar(pkl[:, :], T.jl[:, 0:width], num[:, 1:2], None, A.add), ["jl", "shift%d" % t], ["pk%d" % n])
+        do("v", lambda e: e.tensor_scalar(pkl[:, :], T.jl[:, 0:width], num[:, 4:5], None, A.add), ["jl", "shift%d" % t], ["pk%d" % n])
         if t < R - 1:
             src, dst = ("cc%d" % n, "cs_%d" % n, 0, STEP + NB), ("sc%d" % n, "ss%d" % n, 0, NB)
-            for q, nm in (("v", "c"), ("a", "s")):
-                pick(q, dst, src, pkl[:, :], ["nc%s%d" % (nm, n), "wc%s%d" % (nm, n), "pk%d" % n], ["snd%s%d" % (nm, n)])
+            for nm in ("c", "s"):
+                pick("a", nm, dst, src, pkl[:, :], ["nc%s%d" % (nm, n), "wc%s%d" % (nm, n), "pk%d" % n], ["snd%s%d" % (nm, n)])
             send(n)
+            wn = later(n)
             lo = LC * (t + 2)
             wid = AL + TC - lo
             tmp, lu, sm = T["tmp%d" % t], T["lu%d" % t], T["sum%d" % t]
-            do("v", lambda e: e.tensor_scalar(tmp[:, 0:wid], sm[:, 16 * LC + 15:16 * (LC + wid):16], num[:, 1:2], 1.0 / STEP, A.mult, A.mult), ["sum%da" % t, "sum%db" % t, "shift%d" % t], ["tmp%d" % t])
+            do("v", lambda e: e.tensor_scalar(tmp[:, 0:wid], sm[:, 16 * LC + 15:16 * (LC + wid):16], num[:, 4:5], 1.0 / STEP, A.mult, A.mult), ["sum%da" % t, "sum%db" % t, "shift%d" % t], ["tmp%d" % t])
+            next(wn)
             do("v", lambda e: e.tensor_tensor(T.lists[:, lo:AL + TC], T.lists[:, lo:AL + TC], tmp[:, 0:wid], A.max), ["tmp%d" % t, "lista", "listb"], ["lista", "listb"])
+            next(wn)
             do("v", lambda e: e.tensor_copy(lu[:, lo:AL + TC], T.lists[:, lo:AL + TC]), ["lista", "listb"], ["lu%d" % t])
-            tab = ("tc%d" % t, "ts%d" % t, 0, K) if t < R - 2 else ("ttc", "tts", 0, K)
-            for q, nm in (("v", "c"), ("a", "s")):
-                pick(q, tab, win, lu[:, AL:AL + TC], held(nm) + ["lu%d" % t], ["tab%s%d" % (nm, t)])
             for i in [t] + ([n] if t == R - 2 else []):
                 a, b = 128 * O * i, 128 * O * (i + 1)
                 do("v", lambda e: e.quantize_mx(T.wc[:, a:b], T.ws[:, a:b], T.wt[:, 4 * a:4 * b]), ["w%d" % i], ["wq%d" % i])
+            tab = ("tc%d" % t, "ts%d" % t, 0, K) if t < R - 2 else ("ttc", "tts", 0, K)
+            for nm in ("c", "s"):
+                pick("a", nm, tab, win, lu[:, AL:AL + TC], held(nm) + ["lu%d" % t], ["tab%s%d" % (nm, t)])
             for o in range(O):
                 i = O * t + o
                 pb = 512 * (i % 4)
@@ -328,16 +342,20 @@ def rank_program(g, core, T, topo):
                 do("a", lambda e: e.activation(T.ty[:, K * i:K * i + K], T.prod[:, pb:pb + K], F.Copy), ["prod%d" % (i % 4)], ["ty%d" % i])
             if n + 1 < R:
                 fetch(n + 1)
+            if k + 2 <= R:
+                carry("co", k + 2, K, end, lambda x: ["sent%d" % n] + past(x, k + 1))
             y = slice(O * K * t, O * K * (t + 1))
             dma("s", "yo%d" % t, T.y[:, y], T.ty[:, y], ["sent%d" % n, "ty%d" % (O * t), "ty%d" % (O * t + 1)], ["out%d" % t])
-            later(n)
+            next(wn)
             quantise(k + 1)
             if t < R - 2:
-                newer(n + 1)
                 m = n + 1
-                wn = ("pc%d" % (k + 1), "ps%d" % (k + 1), 0, end)
-                for q, nm in (("v", "c"), ("a", "s")):
-                    pick(q, ("cc%d" % m, "cs_%d" % m, 0, NB), wn, lu[:, LC * m:LC * m + LC], ["own%s%d" % (nm, k + 1), "cp%s%d" % (nm, k + 1), "lu%d" % t], ["nc%s%d" % (nm, m)])
+                nw = newer(m)
+                next(nw)
+                src = ("pc%d" % (k + 1), "ps%d" % (k + 1), 0, end)
+                for nm in ("c", "s"):
+                    pick("a", nm, ("cc%d" % m, "cs_%d" % m, 0, NB), src, lu[:, LC * m:LC * m + LC], ["own%s%d" % (nm, k + 1), "lu%d" % t] + past(nm, k + 1), ["nc%s%d" % (nm, m)])
+                next(nw)
             else:
                 do("v", lambda e: e.tensor_tensor(T.fcf[:, :], T.lists[:, AL:AL + TC], T["sum%d" % n][:, 15:16 * TC:16], A.max), ["listb", "sum%db" % n], ["fcf"])
                 do("v", lambda e: e.tensor_copy(T.fcu[:, :], T.fcf[:, :]), ["fcf"], ["fcu"])
@@ -345,8 +363,8 @@ def rank_program(g, core, T, topo):
             H = K // 2
             for h in range(2):
                 tab = ("tc%d" % t, "ts%d" % t, H * h, H * h + H)
-                for q, nm in (("v", "c"), ("a", "s")):
-                    pick(q, tab, ("ttc", "tts", 0, 2 * K), pkl[:, TC // 2 * h:TC // 2 * (h + 1)], ["tab%s%d" % (nm, t - 1), "wc%s%d" % (nm, n), "pk%d" % n], ["tab%s%d%d" % (nm, t, h)])
+                for nm in ("c", "s"):
+                    pick("a", nm, tab, ("ttc", "tts", 0, 2 * K), pkl[:, TC // 2 * h:TC // 2 * (h + 1)], ["tab%s%d" % (nm, t - 1), "wc%s%d" % (nm, n), "pk%d" % n], ["tab%s%d%d" % (nm, t, h)])
                 for o in range(O):
                     i = O * t + o
                     pb = 512 * (2 * h + o)

from concourse.bass import DstId, RemoteDMATransfer
from concourse.mybir import dt, AluOpType, ActivationFunctionType

N, K, B, R, O = 8, 256, 12, 5, 2
NB = N * B
NEW = (N - 1) * B
LC = NB // 16
TC = K // 16
AL = R * LC
WIN = K + 16
STEP = 128
TINY = 1e-30

CODE, BYTE = "float8_e4m3fn_x4", "uint8"
SCRATCH = {
    "xt": ("sbuf", [128, 4 * K], "bfloat16"),
    "ut": ("sbuf", [128, 512], "bfloat16"),
    "wt": ("sbuf", [128, 512 * R * O], "bfloat16"),
    "csl": ("sbuf", [128, AL], "int32"),
    "cdl": ("sbuf", [128, AL], "int32"),
    "thr1": ("sbuf", [1, 16], "int32"),
    "thri": ("sbuf", [128, 16], "int32"),
    "thrf": ("sbuf", [128, 16], "float32"),
    "csu": ("sbuf", [128, AL], "uint16"),
    "cdo": ("sbuf", [128, AL], "uint16"),
    "own1": ("sbuf", [128, AL], "float32"),
    "own2": ("sbuf", [128, AL], "float32"),
    "cdf": ("sbuf", [128, AL], "float32"),
    "trash": ("sbuf", [128, AL], "float32"),
    "trash2": ("sbuf", [128, AL], "float32"),
    "pp": ("sbuf", [128, 2], "int32"),
    "p16": ("sbuf", [128, 2], "int32"),
    "p16f": ("sbuf", [128, 2], "float32"),
    "run": ("sbuf", [128, 384], "float32"),
    "mask": ("sbuf", [128, 384], "float32"),
    "seg": ("sbuf", [128, 384], "float32"),
    "jc": ("sbuf", [128, TC], "float32"),
    "jl": ("sbuf", [128, TC], "float32"),
    "vrow": ("sbuf", [128, NB], "float32"),
    "inv": ("sbuf", [128, R * WIN], "float32"),
    "lists": ("sbuf", [128, AL + TC], "float32"),
    "zeros": ("sbuf", [128, 8], "uint16"),
    "uc": ("sbuf", [128, 128], CODE), "us": ("sbuf", [128, 128], BYTE),
    "vc": ("sbuf", [128, 128], CODE), "vs": ("sbuf", [128, 128], BYTE),
    "wc": ("sbuf", [128, 128 * R * O], CODE), "ws": ("sbuf", [128, 128 * R * O], BYTE),
    "ttc": ("sbuf", [128, 2 * K], CODE), "tts": ("sbuf", [128, 2 * K], BYTE),
    "ty": ("sbuf", [128, R * O * K], "float32"),
    "acc": ("psum", [128, 1024], "float32"),
    "prod": ("psum", [128, 2048], "float32"),
    "fcf": ("sbuf", [128, TC], "float32"),
    "fcu": ("sbuf", [128, TC], "uint16"),
    "pkl": ("sbuf", [128, TC], "uint16"),
}
for _k in range(R + 1):
    SCRATCH["pc%d" % _k] = ("sbuf", [128, K + NEW * _k], CODE)
    SCRATCH["ps%d" % _k] = ("sbuf", [128, K + NEW * _k], BYTE)
for _t in range(R):
    SCRATCH["sc%d" % _t] = ("sbuf", [128, NB], CODE)
    SCRATCH["ss%d" % _t] = ("sbuf", [128, NB], BYTE)
    SCRATCH["val%d" % _t] = ("sbuf", [128, NB], "float32")
    SCRATCH["lin%d" % _t] = ("sbuf", [128, 640], "float32")
    SCRATCH["sum%d" % _t] = ("sbuf", [128, 640], "float32")
    SCRATCH["bit%d" % _t] = ("sbuf", [128, NEW], "bfloat16")
    SCRATCH["num%d" % _t] = ("sbuf", [128, 8], "float32")
    SCRATCH["tmp%d" % _t] = ("sbuf", [128, AL + TC], "float32")
    SCRATCH["lu%d" % _t] = ("sbuf", [128, AL + TC], "uint16")
    if _t:
        SCRATCH["cc%d" % _t] = ("sbuf", [128, STEP + NB], CODE)
        SCRATCH["cs_%d" % _t] = ("sbuf", [128, STEP + NB], BYTE)
        SCRATCH["ncf%d" % _t] = ("sbuf", [128, LC], "float32")
        SCRATCH["ncu%d" % _t] = ("sbuf", [128, LC], "uint16")
        SCRATCH["pk%d" % _t] = ("sbuf", [128, LC], "uint16")
    if _t < R - 2 or _t == R - 1:
        SCRATCH["tc%d" % _t] = ("sbuf", [128, K], CODE)
        SCRATCH["ts%d" % _t] = ("sbuf", [128, K], BYTE)

SEMAPHORES = ["vq", "aq", "pq", "gq", "lx0", "lx1", "lc0", "lc1", "ld0", "ld1", "lu", "lt", "yp"]
for _t in range(R):
    SEMAPHORES += ["arrc%d" % _t, "arrs%d" % _t, "yo%d" % _t, "snt%d" % _t, "lw%d" % _t]
for _k in range(2, R + 1):
    SEMAPHORES += ["cp%d" % _k]
for _k in range(3, R + 1):
    SEMAPHORES += ["co%d" % _k]


def deal(topo, cores, s):
    src = cores[s]
    home, off = [], []
    for d in range(len(cores)):
        if d != s:
            (home if topo.chip(cores[d]) == topo.chip(src) else off).append(d)
    near = lambda d: topo.mates(topo.chip(src), topo.chip(cores[d])) or topo.same_plane(topo.chip(src), topo.chip(cores[d]))
    eng = topo.engines(src, cores[off[0]])
    even, odd = eng[0::2], eng[1::2]
    two = len(eng) - len(off)
    off = [d for d in off if not near(d)] + [d for d in off if near(d)]
    codes, scales = {}, {}
    for i, d in enumerate(off):
        codes[d] = even[2 * i:2 * i + 2] if i < two else [odd[i - two]]
        scales[d] = odd[2 * i:2 * i + 2] if i < two else [even[i - two]]
    for d in home:
        rest = [e for e in topo.engines(src, cores[d]) if e not in eng]
        codes[d] = scales[d] = rest[::max(1, len(rest) // 2)][:2]
    bits = lambda m: {d: sum(1 << e for e in m[d]) for d in m}
    return bits(codes), bits(scales)


def rank_program(g, core, T, topo):
    r = T.rank_of(core)
    if r is None:
        return
    cores = list(T.cores)
    A, F = AluOpType, ActivationFunctionType
    plans = [deal(topo, cores, s) for s in range(N)]
    ones = lambda m: bin(m).count("1")

    total, W, RD = {}, {}, {}
    qs = {}
    for name, eng, sem in (("v", g.vector, "vq"), ("a", g.scalar, "aq"), ("p", g.tensor, "pq"), ("g", g, "gq"), ("s", g.sync, None)):
        qs[name] = {"eng": eng, "sem": sem, "seen": {}}

    def hold(q, toks):
        need = {}
        for sem, n in toks:
            n = total[sem] if n is None else n
            if qs[q]["seen"].get(sem, 0) < n:
                need[sem] = max(need.get(sem, 0), n)
        for sem in sorted(need):
            qs[q]["eng"].wait_ge(T.sem[sem], need[sem])
            qs[q]["seen"][sem] = need[sem]

    def order(q, rd, wr):
        toks = []
        for k in rd:
            toks += W[k]
        for k in wr:
            toks += W.get(k, []) + RD.get(k, [])
        hold(q, toks)

    def note(tok, rd, wr):
        for k in rd:
            RD.setdefault(k, []).append(tok)
        for k in wr:
            W[k] = [tok]
            RD[k] = []

    def do(q, make, rd, wr):
        order(q, rd, wr)
        sem = qs[q]["sem"]
        make(qs[q]["eng"]).then_inc(T.sem[sem], 1)
        total[sem] = total.get(sem, 0) + 1
        note((sem, total[sem]), rd, wr)

    def dma(q, sem, out, in_, rd, wr):
        order(q, rd, [])
        qs[q]["eng"].dma_start(out, in_).then_inc(T.sem[sem], 16)
        total[sem] = total.get(sem, 0) + 16
        tok = (sem, None)
        for k in rd:
            RD.setdefault(k, []).append(tok)
        for k in wr:
            if tok not in W.setdefault(k, []):
                W[k].append(tok)

    for t in range(R):
        for h, nm in ((0, "c"), (1, "s")):
            sem = "arr%s%d" % (nm, t)
            total[sem] = sum(ones(plans[s][h][r]) for s in range(N) if s != r)
            W["land%s%d" % (nm, t)] = [(sem, None)]
        W["sent%d" % t] = [("snt%d" % t, None)]

    h = 2 * K
    dma("s", "lx0", T.xt[:, 0:h], T.x[:, 0:h], [], ["x"])
    dma("a", "lx1", T.xt[:, h:2 * h], T.x[:, h:2 * h], [], ["x"])
    for i in range(8):
        q, n = ("s", "0") if i < 4 else ("a", "1")
        dma(q, "lc" + n, T.csl[16 * i:16 * i + 16, :], T.cs[:, :], [], ["cs"])
    dma("s", "lu", T.ut[:, :], T.u[:, :], [], ["u"])
    for i in range(8):
        q, n = ("s", "0") if i < 4 else ("a", "1")
        dma(q, "ld" + n, T.cdl[16 * i:16 * i + 16, :], T.cd[:, :], [], ["cd"])
    dma("s", "lt", T.thr1[0:1, :], T.thr[:, :], [], ["thr1"])

    fl = {"allow_small_or_imprecise_dtypes": True}
    do("g", lambda e: e.iota(T.pp[:, 0:1], [[0, 1]], 0, 1), [], ["pp"])
    do("g", lambda e: e.iota(T.run[:, :], [[0, 24], [1, 16]], 0, 0, **fl), [], ["run"])
    do("g", lambda e: e.iota(T.jc[:, :], [[16, TC]], 0, 0, **fl), [], ["jc"])
    do("g", lambda e: e.iota(T.trash[:, :], [[0, R], [16, LC]], K + 1 - B * r, 0, **fl), [], ["trash"])
    do("g", lambda e: e.iota(T.vrow[:, 0:B * (r + 1)], [[1, B * (r + 1)]], 0, 0, **fl), [], ["vrowa"])
    W["vrowb"] = []
    if r < N - 1:
        do("g", lambda e: e.iota(T.vrow[:, B * (r + 1):NB], [[1, NB - B * (r + 1)]], B * r, 0, **fl), [], ["vrowb"])
    do("v", lambda e: e.memset(T.zeros[:, :], 0), [], ["zeros"])
    for i in range(R):
        do("v", lambda e: e.memset(T.inv[:, WIN * i:WIN * i + K], 0.0), [], ["inv%d" % i])
    col = T.p16f[:, 0:1]
    do("v", lambda e: e.tensor_scalar(T.p16[:, 0:1], T.pp[:, 0:1], 15, None, A.bitwise_and), ["pp"], ["p16"])
    do("v", lambda e: e.tensor_copy(T.p16f[:, 0:1], T.p16[:, 0:1]), ["p16"], ["p16f"])
    do("v", lambda e: e.tensor_scalar(T.mask[:, :], T.run[:, :], col, None, A.is_equal), ["run", "p16f"], ["mask"])
    do("v", lambda e: e.tensor_scalar(T.jl[:, :], T.jc[:, :], col, None, A.add), ["jc", "p16f"], ["jl"])
    do("v", lambda e: e.tensor_scalar(T.trash2[:, :], T.trash[:, :], col, None, A.add), ["trash", "p16f"], ["trash2"])
    do("v", lambda e: e.tensor_copy(T.lists[:, AL:AL + TC], T.jl[:, :]), ["jl"], ["listb"])

    def quantise(k):
        do("v", lambda e: e.quantize_mx(T["pc%d" % k][:, 0:K], T["ps%d" % k][:, 0:K], T.xt[:, :]), ["x"], ["ownc%d" % k, "owns%d" % k])

    def pick(q, nm, out, win, off, rd, wr):
        if nm == "c":
            do("v", lambda e: e.tensor_copy(T[out[0]][:, out[2]:out[3]].bitcast(dt.uint32), T[win[0]][:, win[2]:win[3]].bitcast(dt.uint32).indirect(off)), rd, wr)
        elif q == "v":
            do("v", lambda e: e.tensor_copy(T[out[1]][:, out[2]:out[3]], T[win[1]][:, win[2]:win[3]].indirect(off)), rd, wr)
        else:
            do("a", lambda e: e.activation(T[out[1]][:, out[2]:out[3]], T[win[1]][:, win[2]:win[3]].indirect(off), F.Copy), rd, wr)

    def send(t):
        codes, scales = plans[r]
        for nm, m, scale in (("c", codes, False), ("s", scales, True)):
            order("g", ["snd%s%d" % (nm, t)], [])
            moves = []
            for d in sorted(m):
                rid, pid, _ring = topo.addr(cores[d])
                a = K + NEW * t + B * (r - (r > d))
                src = T["s%s%d" % (nm, t)][:, B * d:B * d + B]
                dst = T["p%s%d" % (nm, t + 1)][:, a:a + B]
                if not scale:
                    src, dst = src.bitcast(dt.uint8), dst.bitcast(dt.uint8)
                moves.append(RemoteDMATransfer(dst_ids=[DstId(rid=rid, pnc=pid)], dma_engine_mask=m[d], remote_sem=T.sem["arr%s%d" % (nm, t)], src=src, dst=dst))
            sem = "snt%d" % t
            g.remote_dma_fused(moves, local_sem=T.sem[sem])
            total[sem] = total.get(sem, 0) + sum(ones(m[d]) for d in m)

    def fetch(t):
        a, b = 512 * O * t, 512 * O * (t + 1)
        dma("s", "lw%d" % t, T.wt[:, a:b], T.w[:, a:b], ["sent%d" % max(t - 1, 0)], ["w%d" % t])

    def carry(name, k, a, b, rd):
        for nm in ("c", "s"):
            o, i = T["p%s%d" % (nm, k)][:, a:b], T["p%s%d" % (nm, k - 1)][:, a:b]
            if nm == "c":
                o, i = o.bitcast(dt.uint8), i.bitcast(dt.uint8)
            dma("s", "%s%d" % (name, k), o, i, rd(nm), ["%s%s%d" % (name, nm, k)])

    quantise(0)
    do("v", lambda e: e.tensor_copy(T.csu[:, :], T.csl[:, :]), ["cs"], ["csu"])
    for nm in ("c", "s"):
        pick("a", nm, ("sc0", "ss0", 0, NB), ("pc0", "ps0", 0, K), T.csu[:, 0:LC], ["own%s0" % nm, "csu"], ["snd%s0" % nm])
    send(0)
    fetch(0)
    fetch(1)
    do("g", lambda e: e.partition_broadcast(T.thri[:, :], T.thr1[0:1, :], 128), ["thr1"], ["thri"])

    def later(t):
        v, s, l, a = "val%d" % t, "sum%d" % t, "lin%d" % t, WIN * t
        n = NB * (R - 1 - t)
        do("v", lambda e: e.tensor_scalar(T[v][:, :], T.vrow[:, :], float(K + NEW * t), None, A.add), ["vrowa", "vrowb"], [v])
        yield
        do("v", lambda e: e.tensor_copy(T.inv[:, a:a + WIN].indirect(T.cdo[:, LC * t:LC * t + LC]), T[v][:, :]), [v, "cdo"], ["inv%d" % t])
        yield
        if n:
            do("v", lambda e: e.tensor_tensor(T[l][:, 0:n], T.inv[:, a:a + K].indirect(T.csu[:, LC * (t + 1):AL]), T.mask[:, 0:n], A.mult), ["inv%d" % t, "csu", "mask"], [l + "a"])
        do("v", lambda e: e.tensor_tensor(T[l][:, n:n + K], T.inv[:, a:a + K], T.mask[:, 0:K], A.mult), ["inv%d" % t, "mask"], [l + "b"])
        if n:
            do("v", lambda e: e.tensor_tensor_scan(T[s][:, 0:n], T.seg[:, 0:n], T[l][:, 0:n], 0.0, A.mult, A.add), ["seg", l + "a"], [s + "a"])
        do("v", lambda e: e.tensor_tensor_scan(T[s][:, n:n + K], T.seg[:, 0:K], T[l][:, n:n + K], 0.0, A.mult, A.add), ["seg", l + "b"], [s + "b"])
        yield

    def newer(t):
        do("v", lambda e: e.tensor_tensor(T["ncf%d" % t][:, :], T.lists[:, LC * t:LC * t + LC], T["sum%d" % (t - 1)][:, 15:16 * LC:16], A.max), ["lista", "sum%da" % (t - 1)], ["ncf%d" % t])
        yield
        do("v", lambda e: e.tensor_copy(T["ncu%d" % t][:, :], T["ncf%d" % t][:, :]), ["ncf%d" % t], ["ncu%d" % t])
        yield

    w0, n1 = later(0), newer(1)
    quantise(1)
    do("v", lambda e: e.tensor_scalar(T.own1[:, :], T.cdl[:, :], 0.0, None, A.is_lt), ["cd"], ["own1"])
    do("v", lambda e: e.quantize_mx(T.uc[:, :], T.us[:, :], T.ut[:, :]), ["u"], ["uc", "us"])
    do("v", lambda e: e.tensor_tensor(T.own2[:, :], T.own1[:, :], T.trash2[:, :], A.mult), ["own1", "trash2"], ["own2"])
    for nm in ("c", "s"):
        pick("a", nm, ("vc", "vs", 0, 128), ("uc", "us", 0, 128), T.zeros[:, :], ["u" + nm, "zeros"], ["v" + nm])
    do("v", lambda e: e.tensor_tensor(T.cdf[:, :], T.cdl[:, :], T.own2[:, :], A.add), ["cd", "own2"], ["cdf"])
    for nm in ("c", "s"):
        pick("a", nm, ("cc1", "cs_1", 0, NB), ("pc1", "ps1", 0, K), T.csu[:, LC:2 * LC], ["own%s1" % nm, "csu"], ["nc%s1" % nm])
    do("v", lambda e: e.tensor_copy(T.cdo[:, :], T.cdf[:, :]), ["cdf"], ["cdo"])
    next(w0)
    do("v", lambda e: e.tensor_scalar(T.lists[:, 0:AL], T.csl[:, :], 0.0, None, A.max), ["cs"], ["lista"])
    next(w0)
    do("v", lambda e: e.tensor_scalar(T.seg[:, :], T.run[:, :], 0.5, None, A.is_gt), ["run"], ["seg"])
    next(w0)
    next(n1)
    do("v", lambda e: e.tensor_scalar(T.thrf[:, :], T.thri[:, :], 2.0, float(-NEW), A.mult, A.add), ["thri"], ["thrf"])
    next(n1)

    for t in range(R):
        k = n = t + 1
        end = K + NEW * k
        num, bit = T["num%d" % t], T["bit%d" % t]
        past = lambda x, j: (["cp%s%d" % (x, j)] if j > 1 else []) + (["co%s%d" % (x, j)] if j > 2 else [])
        held = lambda x: ["own%s%d" % (x, k), "land%s%d" % (x, t)] + past(x, k)
        if t < R - 1:
            carry("cp", k + 1, end - NEW, end, lambda x: ["land%s%d" % (x, t)])
        sb = 512 * (t % 2)
        do("p", lambda e: e.matmul_mx(T.acc[:, sb:sb + 128], T.vc[:, :], T.vs[:, :], T["pc%d" % k][:, end - 128:end], T["ps%d" % k][:, end - 128:end], True, True), ["vc", "vs"] + held("c") + held("s"), ["acc%d" % (t % 2)])
        if t < R - 1:
            out, off, cv = ("cc%d" % n, "cs_%d" % n, STEP, STEP + NB), T["ncu%d" % n][:, :], "ncu%d" % n
        else:
            out, off, cv = ("ttc", "tts", K, 2 * K), T.fcu[:, :], "fcu"
        win = ("pc%d" % k, "ps%d" % k, 0, end)
        for nm in ("c", "s"):
            pick("v", nm, out, win, off, held(nm) + [cv], ["wc%s%d" % (nm, n)])
        do("a", lambda e: e.activation(bit[:, :], T.acc[:, sb + 128 - NEW:sb + 128], F.Sign, bias=TINY, accum_out=num[:, 0:1]), ["acc%d" % (t % 2)], ["cnt%d" % t])
        step, width = (STEP, LC) if t < R - 1 else (K, TC)
        do("v", lambda e: e.tensor_scalar(num[:, 4:5], num[:, 0:1], T.thrf[:, t:t + 1], float(step), A.is_ge, A.mult), ["cnt%d" % t, "thrf"], ["shift%d" % t])
        pkl = T["pk%d" % n] if t < R - 1 else T.pkl
        do("v", lambda e: e.tensor_scalar(pkl[:, :], T.jl[:, 0:width], num[:, 4:5], None, A.add), ["jl", "shift%d" % t], ["pk%d" % n])
        if t < R - 1:
            src, dst = ("cc%d" % n, "cs_%d" % n, 0, STEP + NB), ("sc%d" % n, "ss%d" % n, 0, NB)
            for nm in ("c", "s"):
                pick("a", nm, dst, src, pkl[:, :], ["nc%s%d" % (nm, n), "wc%s%d" % (nm, n), "pk%d" % n], ["snd%s%d" % (nm, n)])
            send(n)
            wn = later(n)
            lo = LC * (t + 2)
            wid = AL + TC - lo
            tmp, lu, sm = T["tmp%d" % t], T["lu%d" % t], T["sum%d" % t]
            do("v", lambda e: e.tensor_scalar(tmp[:, 0:wid], sm[:, 16 * LC + 15:16 * (LC + wid):16], num[:, 4:5], 1.0 / STEP, A.mult, A.mult), ["sum%da" % t, "sum%db" % t, "shift%d" % t], ["tmp%d" % t])
            next(wn)
            do("v", lambda e: e.tensor_tensor(T.lists[:, lo:AL + TC], T.lists[:, lo:AL + TC], tmp[:, 0:wid], A.max), ["tmp%d" % t, "lista", "listb"], ["lista", "listb"])
            next(wn)
            do("v", lambda e: e.tensor_copy(lu[:, lo:AL + TC], T.lists[:, lo:AL + TC]), ["lista", "listb"], ["lu%d" % t])
            for i in [t] + ([n] if t == R - 2 else []):
                a, b = 128 * O * i, 128 * O * (i + 1)
                do("v", lambda e: e.quantize_mx(T.wc[:, a:b], T.ws[:, a:b], T.wt[:, 4 * a:4 * b]), ["w%d" % i], ["wq%d" % i])
            tab = ("tc%d" % t, "ts%d" % t, 0, K) if t < R - 2 else ("ttc", "tts", 0, K)
            for nm in ("c", "s"):
                pick("a", nm, tab, win, lu[:, AL:AL + TC], held(nm) + ["lu%d" % t], ["tab%s%d" % (nm, t)])
            for o in range(O):
                i = O * t + o
                pb = 512 * (i % 4)
                do("p", lambda e: e.matmul_mx(T.prod[:, pb:pb + K], T.wc[:, 128 * i:128 * i + 128], T.ws[:, 128 * i:128 * i + 128], T[tab[0]][:, 0:K], T[tab[1]][:, 0:K], True, True), ["wq%d" % t, "tabc%d" % t, "tabs%d" % t], ["prod%d" % (i % 4)])
            for o in range(O):
                i = O * t + o
                pb = 512 * (i % 4)
                do("a", lambda e: e.activation(T.ty[:, K * i:K * i + K], T.prod[:, pb:pb + K], F.Copy), ["prod%d" % (i % 4)], ["ty%d" % i])
            if n + 1 < R:
                fetch(n + 1)
            if k + 2 <= R:
                carry("co", k + 2, K, end, lambda x: ["sent%d" % n] + past(x, k + 1))
            y = slice(O * K * t, O * K * (t + 1))
            dma("s", "yo%d" % t, T.y[:, y], T.ty[:, y], ["sent%d" % n, "ty%d" % (O * t), "ty%d" % (O * t + 1)], ["out%d" % t])
            next(wn)
            quantise(k + 1)
            if t < R - 2:
                m = n + 1
                nw = newer(m)
                next(nw)
                src = ("pc%d" % (k + 1), "ps%d" % (k + 1), 0, end)
                for nm in ("c", "s"):
                    pick("a", nm, ("cc%d" % m, "cs_%d" % m, 0, NB), src, lu[:, LC * m:LC * m + LC], ["own%s%d" % (nm, k + 1), "lu%d" % t] + past(nm, k + 1), ["nc%s%d" % (nm, m)])
                next(nw)
            else:
                do("v", lambda e: e.tensor_tensor(T.fcf[:, :], T.lists[:, AL:AL + TC], T["sum%d" % n][:, 15:16 * TC:16], A.max), ["listb", "sum%db" % n], ["fcf"])
                do("v", lambda e: e.tensor_copy(T.fcu[:, :], T.fcf[:, :]), ["fcf"], ["fcu"])
        else:
            H = K // 2
            for h in range(2):
                tab = ("tc%d" % t, "ts%d" % t, H * h, H * h + H)
                for nm in ("c", "s"):
                    pick("a", nm, tab, ("ttc", "tts", 0, 2 * K), pkl[:, TC // 2 * h:TC // 2 * (h + 1)], ["tab%s%d" % (nm, t - 1), "wc%s%d" % (nm, n), "pk%d" % n], ["tab%s%d%d" % (nm, t, h)])
                for o in range(O):
                    i = O * t + o
                    pb = 512 * (2 * h + o)
                    do("p", lambda e: e.matmul_mx(T.prod[:, pb:pb + H], T.wc[:, 128 * i:128 * i + 128], T.ws[:, 128 * i:128 * i + 128], T[tab[0]][:, tab[2]:tab[3]], T[tab[1]][:, tab[2]:tab[3]], True, True), ["wq%d" % t, "tabc%d%d" % (t, h), "tabs%d%d" % (t, h)], ["prod%d" % (2 * h + o)])
            for h in range(2):
                for o in range(O):
                    a, pb = K * (O * t + o) + H * h, 512 * (2 * h + o)
                    y = slice(a, a + H)
                    if o:
                        do("a", lambda e: e.activation(T.ty[:, y], T.prod[:, pb:pb + H], F.Copy), ["prod%d" % (2 * h + o)], ["tyz%d%d" % (h, o)])
                    else:
                        do("v", lambda e: e.tensor_copy(T.ty[:, y], T.prod[:, pb:pb + H]), ["prod%d" % (2 * h + o)], ["tyz%d%d" % (h, o)])
                    q, sem = ("a", "yp") if o and h else ("s", "yo%d" % t)
                    dma(q, sem, T.y[:, y], T.ty[:, y], ["tyz%d%d" % (h, o)], ["outz%d%d" % (h, o)])

    hold("g", [(sem, None) for sem in sorted(total)])
